import numpy as np, ml_dtypes
CORES = [36,164,52,180,100,228,116,244]
N = 8
BF = ml_dtypes.bfloat16
LN, B, SQ, KN, RO, SH = 256, 2, 128, 16, 5, 6
KS = KN * SQ; W = B * KS
def draw(rng):
    fe = np.clip(rng.integers(-6, 10, (N, 8, 16, 1, 1, 1), dtype=np.int8) + rng.integers(-3, 4, (N, 8, 1, 1, KN, 1), dtype=np.int8) + rng.integers(-9, 10, (N, 8, 16, B, KN, SQ), dtype=np.int8), -15, 15)
    kind = rng.integers(1, KN, (N, 8, 16, LN)); sq = rng.integers(0, SQ, (N, 8, 16, LN)); gone = rng.random((N, 8, 16, LN)) < 0.2
    near = (rng.integers(0, SQ, (1, 8, LN)) + rng.integers(0, 3, (N, 8, LN))) & (SQ - 1)
    sq[:, :, 0] = np.where(rng.random((N, 8, LN)) < 0.7, near, sq[:, :, 0])
    st = rng.integers(1, SQ, (N, 8, 16)); u = rng.integers(-127, 128, (N, 8, 16, 16)); v = rng.integers(-127, 128, (N, 8, 16, 16))
    u[..., 0] = np.where(rng.random((N, 8, 1)) < 0.5, np.abs(u[..., 0]), u[..., 0])
    return fe, kind, sq, gone, st, u, v
def pack(fe, kind, sq, gone, st, u, v):
    fe = fe.copy(); fe[:, :, :, :, 0] = 0
    po = np.where(gone & (np.arange(16) > 0)[None, None, :, None], 0, kind * SQ + sq)
    return {"feat": fe.reshape(N, 128, W).astype(np.float32).astype(BF), "pos": np.ascontiguousarray(po.reshape(N, 128, LN)).astype(np.int32), "step": np.ascontiguousarray(st.reshape(N, 128, 1)).astype(np.int32),
            "u": u.reshape(N, 128, 16).astype(np.float32).astype(BF), "v": v.reshape(N, 128, 16).astype(np.float32).astype(BF)}
def setup_inputs(rng):
    return pack(*draw(rng))
def setup_inputs_ends(rng):
    fe, kind, sq, gone, st, u, v = draw(rng); mode = np.array([0, 1, 2, 0, 1, 2, 1, 2])
    fe = (30 * rng.integers(0, 2, (N, 8, 16, B, KN, SQ), dtype=np.int8) - 15).astype(np.int8)
    fe[:, mode == 1] = (30 * rng.integers(0, 2, (N, 3, 1, B, KN, SQ)) - 15).astype(np.int8)
    kind[:] = KN - 1; sq[:] = SQ - 1; gone = rng.random(gone.shape) < 0.5
    low = rng.random((N, 8, LN)) < 0.5; kind[:, :, 0] = np.where(low, 1, KN - 1); sq[:, :, 0] = np.where(low, 0, SQ - 1)
    st = np.where(rng.random(st.shape) < 0.5, 1, SQ - 1); st[:, 0, 0] = 1; st[:, 0, 1] = SQ - 1
    u = 254 * rng.integers(0, 2, u.shape) - 127; v = 254 * rng.integers(0, 2, v.shape) - 127
    u[:, mode == 1] = 254 * rng.integers(0, 2, (N, 3, 1, 16)) - 127; v[:, mode == 1] = 254 * rng.integers(0, 2, (N, 3, 1, 16)) - 127
    for q in range(N):
        for g in (2, 5, 7):
            mine = KN - 1 - (q & 1); other = KN - 2 + (q & 1)
            fe[q, g, :, :, mine] = -15; fe[q, g, :, :, other] = 15; fe[q, g, :, :, KN - 3] = 14
            kind[q, g, :, 3::4] = mine; sq[q, g, :, 3::4] = SQ - 1 - (q & 1); gone[q, g, :, 3::4] = False
            w = np.arange(3, LN, 8); w = w[(((w >> 3) + q) & 1) == 1]; kind[q, g, 0, w] = KN - 3
            sq[q, g, 0, 15::16] = SQ - 1 if q == N - 2 else (B - 1) << SH if q == N - 1 else 1 << (SH - 1)
            st[q, g, 0] = SQ - 1
            u[q, g] = -127; u[q, g][:, [5, 10, 15, int(rng.integers(1, 15))]] = 127
            v[q, g] = 254 * rng.integers(0, 2, (1, 16)) - 127; v[q, g, :, 0] = -127; v[q, g][:, [7, 15]] = 127
    return pack(fe, kind, sq, gone, st, u, v)
def setup_inputs_corners(rng):
    fe, kind, sq, gone, st, u, v = draw(rng); i = np.arange(LN); c = i % 8
    st[:, 1::2] = st[:, 1::2, 0:1]
    edge = ((rng.integers(0, B, (N, 8, 1, LN)) << SH) - rng.integers(0, 2, (N, 8, 1, LN))) & (SQ - 1)
    k0 = np.where(c == 3, edge, sq[:, :, 0:1]); s0 = st[:, :, 0][:, :, None, None]; q = sq[:, :, 1:].copy()
    sm = np.take_along_axis(st, rng.integers(0, 16, (N, 8, 15 * LN)), 2).reshape(N, 8, 15, LN)
    q = np.where((c == 1) | (c == 6), k0, q); q = np.where(c == 2, k0 + s0, q)
    q = np.where(c == 4, k0 + s0 * rng.integers(0, 2, q.shape), q); q = np.where(c == 5, k0 - sm, q)
    sq = np.concatenate([k0, q & (SQ - 1)], axis=2)
    but = (c == 2) & ((i >> 3) % 2 == 1); sq[:, :, 15] = np.where(but, (sq[:, :, 15] + 1) & (SQ - 1), sq[:, :, 15])
    kind = np.where(c == 6, kind[:, :, 0:1], kind)
    gone = np.where(c == 0, True, np.where((c == 3) | (c == 7), gone, False))
    fe[:, 4] = -np.abs(fe[:, 4]); fe[:, 6] = np.abs(fe[:, 6])
    u[:, 0:2] = np.minimum(u[:, 0:2], 126); u[:, 0:2, :, 0] = 127
    u[:, 7, :, 8:] = u[:, 7, :, :8]; v[:, 7, :, 8:] = v[:, 7, :, :8]; v[:, 2, :, 8:] = v[:, 2, :, :8]
    return pack(fe, kind, sq, gone, st, u, v)
def setup_inputs_calm(rng):
    fe, kind, sq, gone, st, u, v = draw(rng); i = np.arange(LN)
    kind[:, :, 0] = 1; kind[:, :, 1:] = rng.integers(2, np.where(i % 2 == 0, 9, KN), (N, 8, 15, LN))
    sq = np.moveaxis(np.argsort(rng.random((N, 8, LN, SQ)), axis=-1)[..., :16], 3, 2)
    sq = (sq - sq[:, :, 0:1] + rng.integers(0, SQ, (1, 8, 1, LN)) + rng.integers(0, 3, (N, 8, 1, LN))) & (SQ - 1)
    gone[:, 4:] = False
    fe = rng.integers(-1, 2, (N, 8, 16, B, KN, SQ), dtype=np.int8); fe[:, :, :, :, :9] = 0; fe[:, 4:] += 8
    a = (np.arange(N)[:, None] + np.arange(8)) & 3; brim = (np.arange(8) >= 4)[None, :, None]; half = (np.arange(16) < 8)[None, None, :]
    fe[:, :, :, :, 1, :] = np.where(half, a[:, :, None] + np.where(brim, 6, 0), np.where(brim, 7, 2)).astype(np.int8)[..., None, None]
    t1 = rng.integers(0, 2, (N, 8, 1, 16)); t1[..., 1] = 1 - t1[..., 0]; t2 = rng.integers(0, 2, (N, 8, 1, 16)); t2[..., 1] = 1 - t2[..., 0]
    h = (np.arange(16) < 8)[:, None]
    u = np.where(h, 1 - t1, t1) * rng.integers(1, 16, (N, 8, 1, 1)); v = np.where(h, 1 - t2, t2) * rng.integers(1, 16, (N, 8, 1, 1))
    return pack(fe, kind, sq, gone, st, u, v)
def setup_inputs_spread(rng):
    fe, kind, sq, gone, st, u, v = draw(rng)
    lim = np.array([0, 1, 3, 7, 15], np.int8)[rng.integers(0, 5, (N, 8, 1, B, KN, SQ))]
    fe = np.clip(rng.integers(-15, 16, (N, 8, 16, B, KN, SQ), dtype=np.int8), -lim, lim)
    big = np.array([1, 15, 60, 127])
    lu = big[rng.integers(0, 4, (N, 8, 1, 16))]; lv = big[rng.integers(0, 4, (N, 8, 1, 16))]
    u = np.clip(rng.integers(-127, 128, u.shape), -lu, lu); v = np.clip(rng.integers(-127, 128, v.shape), -lv, lv)
    st = np.minimum(np.exp2(rng.random(st.shape) * (SQ.bit_length() - 1)).astype(np.int64), SQ - 1)
    kind = np.minimum(1 + ((KN - 1) * rng.random(kind.shape) ** 3).astype(np.int64), KN - 1)
    sq[:, ::2] = np.minimum((SQ * rng.random((N, 4, 16, LN)) ** 2).astype(np.int64), SQ - 1)
    gone = rng.random(gone.shape) < rng.random((N, 8, 1, LN))
    return pack(fe, kind, sq, gone, st, u, v)
def steepness(rng, neg):
    t = np.argsort(rng.random((N, 8, 16, 12)), axis=2) & 1
    w = np.concatenate([rng.integers(110, 116, (N, 8, 16, 4)), rng.integers(119, 127, (N, 8, 16, 1)) + t], axis=3)
    return w - np.where(neg, 237, 0)[None, :, None, None]
def setup_inputs_steep(rng):
    fe, kind, sq, gone, st, u, v = draw(rng); g = np.arange(8)
    fe = rng.integers(5, 11, (N, 8, 16, B, KN, SQ), dtype=np.int8); gone = rng.random(gone.shape) < 0.03
    st = 1 + np.argsort(rng.random((N, 8, SQ - 1)), axis=-1)[..., :16]
    u = steepness(rng, (g >> 1) % 2 == 1); v = steepness(rng, g % 2 == 1)
    u[:, 6:] = np.roll(u[:, 6:], -4, axis=3)
    return pack(fe, kind, sq, gone, st, u, v)
def check_inputs(d):
    bad = []
    for k, lo, hi in (("feat", -15, 15), ("pos", 0, KS - 1), ("step", 1, SQ - 1), ("u", -127, 127), ("v", -127, 127)):
        x = np.asarray(d[k]).astype(np.float32)
        if not (np.min(x) >= lo and np.max(x) <= hi): bad.append("range of " + k)
        elif not np.all(x == np.rint(x)): bad.append("whole numbers in " + k)
    p = np.asarray(d["pos"])
    if np.any((p > 0) & (p < SQ)): bad.append("piece numbers of kind 0 in pos")
    if np.any(p[:, ::16] < SQ): bad.append("an empty row 0 in pos")
    if np.any(np.asarray(d["feat"]).reshape(N, 128, B, KN, SQ)[:, :, :, 0].astype(np.float32) != 0): bad.append("columns of kind 0 in feat")
    return bad
def reference(feat, pos, step, u, v):
    fe = feat.astype(np.float32).astype(np.int32).reshape(N, 8, 16, W); st = step.astype(np.int64).reshape(N, 8, 16)
    ut = np.swapaxes(u.astype(np.float32).astype(np.int64).reshape(N, 8, 16, 16), 2, 3); vt = np.swapaxes(v.astype(np.float32).astype(np.int64).reshape(N, 8, 16, 16), 2, 3)
    cur = pos.astype(np.int64).reshape(N, 8, 16, LN)
    cl = np.zeros((N, 8, 16, LN, B), np.int64); ca = np.zeros((N, 8, 16, LN, B), np.int64); row = np.arange(16)[None, None, :, None]
    for t in range(RO):
        if t > 0: cur = np.roll(cur, 1, axis=0)
        b = (cur[:, :, 0] & (SQ - 1)) >> SH
        ix = np.broadcast_to(b[:, :, None, :, None], (N, 8, 16, LN, 1))
        o = np.take_along_axis(cl, ix, 4)[..., 0]; a = np.take_along_axis(ca, ix, 4)[..., 0]; ne = o != cur
        for k in range(16):
            w = np.take_along_axis(fe, (b * KS + o[:, :, k])[:, :, None, :], 3)
            a = np.where(ne[:, :, k][:, :, None, :], np.maximum(a - w, 0), a)
        for k in range(16):
            w = np.take_along_axis(fe, (b * KS + cur[:, :, k])[:, :, None, :], 3)
            a = np.where(ne[:, :, k][:, :, None, :], np.maximum(a + w, 0), a)
        np.put_along_axis(cl, ix, cur[..., None], 4); np.put_along_axis(ca, ix, a[..., None], 4)
        y = np.minimum(a, 127)
        k = np.argmax(np.where(cur > 0, np.matmul(ut, y), -2 ** 40), axis=2); m = np.argmax(np.matmul(vt, y), axis=2)
        old = np.take_along_axis(cur, k[:, :, None, :], 2)[:, :, 0]; s = old & (SQ - 1)
        new = (s + np.take_along_axis(st, m, 2)) & (SQ - 1)
        me = row == k[:, :, None, :]
        hit = (cur > 0) & (row > 0) & ((cur & (SQ - 1)) == new[:, :, None, :])
        cur = np.where(me, (old - s + new)[:, :, None, :], np.where(hit, 0, cur))
    return {"yl": cur.reshape(N, 128, LN).astype(np.float32), "ya": ca.reshape(N, 128, LN * B).astype(np.float32), "yc": cl.reshape(N, 128, LN * B).astype(np.float32)}

@@ -1,0 +1,560 @@
+import numpy as np
+from concourse.bass import DstId, RemoteDMATransfer
+from concourse.mybir import AluOpType, AxisListType, ActivationFunctionType
+
+ALU = AluOpType
+ACT = ActivationFunctionType
+N, LN, PLIES = 8, 256, 5
+NCH, CW = 8, 64
+ND1 = 2
+PAR = {
+    "widths": (64, 64, 64, 64),
+    "banks": "stage",
+    "gat0": (0, 32, 32), "gat1": (4, 16, 40),
+    "early": True,
+    "negv": 1,
+    "scalar": (),
+    "reset": "G",
+    "hop": 0.10, "fix": 0.03, "cyc": 0.001, "gat": 1.56, "pe": 0.0005, "pefix": 0.08, "issue": 0.8, "wire": 2.6,
+    "beat0": 2.2, "beat": 2.6, "kway": 3.0, "look": 0.05, "seed": 0, "noise": 0.0,
+}
+MATS = ["one", "I", "nI", "J", "nJ", "JmI", "nJ4", "Bk", "nBk", "Bk2", "nE", "nQ", "nM", "pM", "U1", "V1", "U4", "V4", "nU4", "nV4"]
+
+SCRATCH = {
+    "tab": ("sbuf", [128, 8192], "bfloat16"),
+    "posi": ("sbuf", [128, LN], "int32"), "sqi": ("sbuf", [128, LN], "int32"), "kni": ("sbuf", [128, LN], "int32"),
+    "uv": ("sbuf", [128, 32], "bfloat16"), "sti": ("sbuf", [128, 8], "int32"), "col": ("sbuf", [128, 8], "float32"),
+    "pi": ("sbuf", [128, 16], "int32"), "pu": ("sbuf", [128, 8], "uint16"),
+    "mat": ("sbuf", [128, 128 * len(MATS)], "bfloat16"),
+    "i32": ("sbuf", [128, 128], "float32"), "sel": ("sbuf", [128, 128], "float32"), "tie": ("sbuf", [128, 128], "float32"),
+    "kin": ("sbuf", [128, PLIES * LN], "bfloat16"),
+    "land": ("sbuf", [128, PLIES * 3 * LN], "bfloat16"), "outb": ("sbuf", [128, 3 * LN], "bfloat16"),
+    "kb": ("sbuf", [128, PLIES * LN], "bfloat16"), "sw": ("sbuf", [128, LN], "bfloat16"), "bb": ("sbuf", [128, LN], "bfloat16"),
+    "eq": ("sbuf", [128, LN], "bfloat16"), "yv": ("sbuf", [128, LN], "bfloat16"), "sth": ("sbuf", [128, LN], "bfloat16"),
+    "wn": ("sbuf", [128, LN], "bfloat16"), "snew": ("sbuf", [128, LN], "bfloat16"),
+    "lst": ("sbuf", [128, PLIES * LN], "float16"), "tl": ("sbuf", [128, (PLIES + 1) * LN], "float16"),
+    "ta": ("sbuf", [128, (PLIES + 1) * LN], "float16"),
+    "off": ("sbuf", [128, 2 * LN], "uint16"),
+    "gw": ("sbuf", [128, 32 * LN], "bfloat16"), "xs": ("sbuf", [128, 32 * LN], "bfloat16"),
+    "x0": ("sbuf", [128, 16 * LN], "bfloat16"),
+    "flo": ("sbuf", [128, ND1 * 32 * CW], "bfloat16"),
+    "pm": ("sbuf", [128, NCH * 128], "float32"), "mxs": ("sbuf", [128, NCH * 128], "float32"),
+    "ol": ("sbuf", [128, LN], "float32"), "oa": ("sbuf", [128, 2 * LN], "float32"), "oc": ("sbuf", [128, 2 * LN], "float32"),
+}
+for _c in range(8):
+    SCRATCH["ps%d" % _c] = ("psum", [128, 512], "float32")
+SEMAPHORES = (["cV", "cA", "cP", "cG", "ldp", "ldw", "ldf", "outs", "karr", "kgo"] + ["go%d" % c for c in range(NCH)]
+              + ["arr%d_%d" % (t, c) for t in range(1, PLIES) for c in range(NCH)])
+STAGE = {"R": 0, "Z": 1, "off": 2, "d1": 3, "sc": 4, "mx": 4, "G": 5, "raw": 6, "yl": 6, "G2": 7, "end": 7}
+SECOND = ("Z", "off", "sc", "G", "end")
+
+
+def bank(stage, c):
+    return "ps%d" % (STAGE[stage] if PAR["banks"] == "stage" else 2 * c + (stage in SECOND))
+
+
+def pieces(n, v, tail, most):
+    parts = []
+    for m, k in ([(n - tail, 0), (tail, v)] if tail else [(n, v)]):
+        a = m - k
+        cnt = -(-a // most)
+        cut = [4 * (a * j // cnt // 4) for j in range(cnt)] + [a]
+        parts.append(([("V", k)] if k else []) + [("A", cut[j + 1] - cut[j]) for j in range(cnt)])
+    return parts
+
+
+def build(g, T, core, topo):
+    rank = T.rank_of(core)
+    ops = []
+    now = [(0, 0, 1)]
+    n = CW
+    W = PAR["widths"]
+    nch = len(W)
+    C0 = [sum(W[:c]) for c in range(nch)]
+    V, S, P = g.vector, g.scalar, g.tensor
+
+    def add(eng, name, cost, reads, writes, fn, banks=(), token=None, after=None):
+        ops.append({"eng": eng, "name": name, "cost": cost, "r": list(reads), "w": list(writes), "fn": fn,
+                    "banks": list(banks), "token": token, "after": after, "chunk": now[0]})
+        return len(ops) - 1
+
+    def M(name):
+        k = MATS.index(name)
+        return T.mat[:, 128 * k:128 * k + 128]
+
+    def vec(name, cyc, reads, writes, fn, banks=()):
+        add("V", name, ("v", max(64, cyc)), reads, writes, fn, banks)
+
+    def act(name, cyc, reads, writes, fn, banks=()):
+        add("A", name, ("v", max(64, cyc)), reads, writes, fn, banks)
+
+    def gps(name, cyc, reads, writes, fn):
+        add("G", name, ("g", cyc), reads, writes, fn)
+
+    def pe(name, groups, reads, bank, begin=True, end=True):
+        def fn():
+            last = None
+            flat = [(out, a, b, k == 0, k == len(terms) - 1) for out, terms in groups for k, (a, b, _) in enumerate(terms)]
+            for k, (out, a, b, s0, s1) in enumerate(flat):
+                if PAR["early"]:
+                    s0, s1 = begin and k == 0, end and k == len(flat) - 1
+                last = P.matmul(out, a, b, s0, s1)
+            return last
+        add("P", name, ("p", sum(x[2] for _, ts in groups for x in ts)), reads + ([] if begin else ["open" + bank]),
+            ([] if end else ["open" + bank]) + ([] if begin else ["shut" + bank]), fn, [bank])
+
+    def pe2(name, groups, k, reads0, reads1, bank):
+        if not PAR["early"]:
+            return pe(name, groups, reads0 + reads1, bank)
+        pe(name + "e", [(o, ts[:-k]) for o, ts in groups], reads0, bank, True, False)
+        pe(name, [(o, ts[-k:]) for o, ts in groups], reads1, bank, False, True)
+
+    def ts(out, in0, s1, op0, s2=None, op1=None):
+        if op1 is None:
+            return lambda: V.tensor_scalar(out, in0, s1, None, op0)
+        return lambda: V.tensor_scalar(out, in0, s1, s2, op0, op1)
+
+    def tt(out, a, b, op):
+        return lambda: V.tensor_tensor(out, a, b, op)
+
+    def scaled(out, in_, k):
+        return lambda: S.activation(out, in_, ACT.Copy, scale=float(k))
+
+    def cols(name, a, b):
+        return ["%s:%d" % (name, k) for k in range(a // 64, (b + 63) // 64)]
+
+    add("S", "ldf", ("d", 5.0), [], ["tab"], lambda: g.sync.dma_start(T.tab[:, 0:4096], T.feat[:]), token=("ldf", 16))
+    add("A", "ldp", ("d", 2.0), [], ["posi"], lambda: S.dma_start(T.posi[:], T.pos[:]), token=("ldp", 16))
+    add("S", "ldu", ("d", 2.0), [], ["u"], lambda: g.sync.dma_start(T.uv[:, 0:16], T.u[:]), token=("ldw", 48))
+    add("S", "ldv", ("d", 2.0), [], ["v"], lambda: g.sync.dma_start(T.uv[:, 16:32], T.v[:]), token=("ldw", 48))
+    add("S", "lds", ("d", 2.0), [], ["sti"], lambda: g.sync.dma_start(T.sti[:, 0:1], T.step[:]), token=("ldw", 48))
+
+    blk = [[-16, 8], [0, 16]]
+    dia = [[-1, 128]]
+    vec("one", 64, [], ["one"], lambda: V.memset(M("one"), 1.0))
+    gps("I", 128, ["one"], ["I"], lambda: g.affine_select(M("I"), M("one"), dia, ALU.is_equal, 0.0, 0, 1))
+    gps("Bk", 128, ["one"], ["Bk"], lambda: g.affine_select(M("Bk"), M("one"), blk, ALU.is_equal, 0.0, 0, 1))
+    gps("J0", 128, ["one"], ["J"], lambda: g.affine_select(M("J"), M("one"), blk, ALU.is_ge, 0.0, 0, 1))
+    gps("J1", 128, ["J"], ["J"], lambda: g.affine_select(M("J"), M("J"), [[16, 8], [0, 16]], ALU.is_ge, 0.0, 15, -1))
+    gps("pi", 8, [], ["pi"], lambda: g.iota(T.pi[:, 0:8], [[0, 8]], 0, 1))
+    gps("sel0", 128, [], ["sel"], lambda: g.iota(T.sel[0:32, :], [[0, 8], [256, 16]], -3840, 0, allow_small_or_imprecise_dtypes=True))
+    gps("sel1", 128, ["sel"], ["sel"], lambda: g.affine_select(T.sel[0:32, :], T.sel[0:32, :], [[0, 128]], ALU.is_ge, 0.0, -8, 1))
+    gps("sel2", 128, ["sel"], ["sel"], lambda: g.affine_select(T.sel[0:32, :], T.sel[0:32, :], [[-1, 8], [0, 16]], ALU.not_equal, 1.0, 0, 1))
+    gps("JmI0", 128, ["J"], ["JmI"], lambda: g.affine_select(M("JmI"), M("J"), dia, ALU.not_equal, 0.0, 0, 1))
+    gps("JmI1", 128, ["JmI"], ["JmI"], lambda: g.affine_select(M("JmI"), M("JmI"), [[-16, 8], [-1000, 16]], ALU.not_equal, 2.0, 0, 1))
+    act("nJ", 128, ["J"], ["nJ"], scaled(M("nJ"), M("J"), -1))
+    gps("nJ4", 128, ["nJ"], ["nJ4"], lambda: g.affine_select(M("nJ4"), M("nJ"), dia, ALU.not_equal, -5.0, 0, 1))
+    gps("Bk2", 128, ["Bk"], ["Bk2"], lambda: g.affine_select(M("Bk2"), M("Bk"), blk, ALU.not_equal, 2.0, -1, 1))
+    for nm, k in (("nE", -4096), ("nI", -1), ("nQ", -16384), ("nM", -2.0 ** 31), ("pM", 2.0 ** 31)):
+        act(nm, 128, ["I"], [nm], scaled(M(nm), M("I"), k))
+    act("i32", 128, ["I"], ["i32"], scaled(T.i32[:], M("I"), 1))
+    act("nBk", 128, ["Bk"], ["nBk"], scaled(M("nBk"), M("Bk"), -1))
+    vec("thr0", 128, ["Bk"], ["thr0"], lambda: V.tensor_reduce(T.col[:, 0:1], M("Bk"), AxisListType.X, ALU.add))
+    vec("thr", 1, ["thr0"], ["thr"], ts(T.col[:, 1:2], T.col[:, 0:1], 12.0, ALU.mult))
+    vec("stf", 1, ["sti"], ["stf"], lambda: V.tensor_copy(T.col[:, 2:3], T.sti[:, 0:1]))
+    vec("pj", 8, ["pi"], ["pj"], ts(T.pi[:, 8:16], T.pi[:, 0:8], 15, ALU.bitwise_and))
+    vec("pu", 8, ["pj"], ["pu"], lambda: V.tensor_copy(T.pu[:], T.pi[:, 8:16]))
+    vec("U1", 250, ["pu", "u", "J"], ["U1"], lambda: V.tensor_tensor(M("U1"), T.uv[:, 0:16].indirect(T.pu[:, 0:8]), M("J"), ALU.mult))
+    vec("V1", 250, ["pu", "v", "J"], ["V1"], lambda: V.tensor_tensor(M("V1"), T.uv[:, 16:32].indirect(T.pu[:, 0:8]), M("J"), ALU.mult))
+    k1, k4, k5 = MATS.index("U1") * 128, MATS.index("U4") * 128, MATS.index("nU4") * 128
+    act("UV4", 256, ["U1", "V1"], ["UV4"], scaled(T.mat[:, k4:k4 + 256], T.mat[:, k1:k1 + 256], 4096))
+    act("nUV4", 256, ["U1", "V1"], ["nUV4"], scaled(T.mat[:, k5:k5 + 256], T.mat[:, k1:k1 + 256], -4096))
+    for k in range(ND1):
+        vec("flo%d" % k, 16 * n, [], cols("flo%d" % k, 0, 32 * n) + ([] if k else ["c240"]),
+            lambda k=k: V.memset(T.flo[:, 32 * n * k:32 * n * (k + 1)], -240.0))
+    vec("tie0", 128, [], ["tie"], lambda: V.memset(T.tie[:], 256.0))
+    vec("tie1", 8, ["tie"], ["tie"], lambda: V.memset(T.tie[:, 0:128:16], -2.0 ** 33))
+    gps("mxs", 128, [], ["mxs0"], lambda: g.iota(T.mxs[0:32, 0:128], [[0, 128]], 1, 0, allow_small_or_imprecise_dtypes=True))
+    gps("mxs", 128, [], ["mxs1"], lambda: g.iota(T.mxs[0:32, 128:256], [[0, 128]], 1, 0, allow_small_or_imprecise_dtypes=True))
+    for b in sorted(set(bank("sc", c) for c in range(nch) if W[c] < 64)):
+        vec("clr" + b, 128, [], [], lambda b=b: V.memset(T[b][:, 0:128], 0.0), [b])
+
+    def land(t, c, what):
+        o, n = (t * LN + C0[c]) * 3, W[c]
+        k = {"S": 0 if t % 2 == 0 else 2, "E": 1, "b": 2 if t % 2 == 0 else 0}[what]
+        return T.land[:, o + k * n:o + (k + 1) * n]
+
+    vec("sqi", LN, ["posi"], ["sqi"], ts(T.sqi[:], T.posi[:], 127, ALU.bitwise_and))
+    vec("kni", LN, ["posi"], ["kni"], ts(T.kni[:], T.posi[:], 1920, ALU.bitwise_and))
+    vec("K0", LN, ["kni"], ["K0"], ts(T.kin[:, 0:LN], T.kni[:], -128.0, ALU.add))
+    for c in range(nch):
+        vec("S0_%d" % c, W[c], ["sqi"], ["S0_%d" % c], ts(land(0, c, "S"), T.sqi[:, C0[c]:C0[c] + W[c]], 128.0, ALU.add))
+        vec("E0_%d" % c, W[c], ["posi"], ["E0_%d" % c], ts(land(0, c, "E"), T.posi[:, C0[c]:C0[c] + W[c]], 0.0, ALU.is_equal))
+
+    def dst(k):
+        rid, pid = topo.addr(T.cores[(rank + k) % N], core)
+        return DstId(rid=rid, pnc=pid)
+
+    wide = topo.mask(core, T.cores[(rank + 1) % N])
+    for k in range(2, PLIES):
+        wide &= topo.mask(core, T.cores[(rank + k) % N])
+    ne = bin(wide).count("1")
+
+    def ksend():
+        tr = RemoteDMATransfer(dst_ids=[dst(k) for k in range(1, PLIES)], dma_engine_mask=wide, remote_sem=T.sem.karr,
+                               src=T.kin[:, 0:LN], dsts=[T.kin[:, k * LN:(k + 1) * LN] for k in range(1, PLIES)])
+        return g.remote_dma_fused([tr], local_sem=T.sem.kgo)
+    ks = add("G", "ksend", ("r", 1), ["K0"], [], ksend, token=("kgo", ne))
+    add("X", "karr", ("x", 2), [], ["K%d" % k for k in range(1, PLIES)], None, token=("karr", ne * (PLIES - 1)), after=ks)
+
+    for k in range(4):
+        a, b = T.tab[:, 4096 + 1024 * k:4096 + 1024 * (k + 1)], T.tab[:, 1024 * k:1024 * (k + 1)]
+        if k < PAR["negv"]:
+            vec("neg%d" % k, 512, ["tab"], ["neg%d" % k], ts(a, b, -1.0, ALU.mult))
+        else:
+            act("neg%d" % k, 1024, ["tab"], ["neg%d" % k], scaled(a, b, -1))
+
+    later = []
+
+    def ply(t, c):
+        last = t == PLIES - 1
+        q = "%d_%d" % (t, c)
+        n, c0 = W[c], C0[c]
+        cs = slice(c0, c0 + n)
+        c240 = T.flo[:, 1:32 * n:32]
+
+        def pl(buf, s):
+            return buf[:, s * LN + c0:s * LN + c0 + n]
+
+        def r(k):
+            return slice(k * n, k * n + n)
+        Sp, Ep, bp, Kp = land(t, c, "S"), land(t, c, "E"), land(t, c, "b"), pl(T.kin, t)
+        rS, rE, rK = "S" + q, "E" + q, "K%d" % t
+        w = 16 if t == 0 else 32
+        g0 = 32 * c0
+
+        def xend(s, i, j):
+            if s == 0:
+                return T.x0[:, 16 * (c0 + i) + 15:16 * (c0 + j):16]
+            return T.xs[:, g0 + 32 * i + 31:g0 + 32 * j:32]
+
+        def rx(s, i, j):
+            return cols("x%d_%d" % (min(s, 1), c), 32 * i, 32 * j)
+        R = [(M("I"), Kp, n), (M("I"), Sp, n), (M("nE"), Ep, n)]
+        rR = [rS, rE, rK, "I", "nE"]
+
+        vec("kb" + q, n // 2, [rS, "thr"], ["kb" + q], ts(pl(T.kb, t), Sp, T.col[:, 1:2], ALU.is_ge, 2048.0, ALU.mult))
+        kb = (M("Bk"), pl(T.kb, t), n)
+        o0 = 2 * c0
+        A, B, O = bank("R", c), bank("Z", c), bank("off", c)
+        pa, pb, po = T[A], T[B], T[O]
+        if t == 0:
+            pe("R" + q, [(pa[:, r(0)], R)], rR, A)
+            pe("offp" + q, [(po[:, r(0)], R + [kb])], rR + ["Bk", "kb" + q], O)
+            vec("off" + q, n, [], ["off%d" % c], lambda: V.tensor_copy(T.off[:, o0:o0 + n], po[:, r(0)]), [O])
+        else:
+            p = "%d_%d" % (t - 1, c)
+            X = pl(T.lst, t - 1)
+            hl = [(M("nI"), pl(T.tl, s), n) for s in range(1, t)]
+            ha = [(M("nI"), pl(T.ta, s), n) for s in range(1, t)]
+            pe("Z" + q, [(pb[:, r(0)], hl + [(M("nI"), X, n)]),
+                         (pb[:, r(1)], ha + [(M("I"), c240, n), (M("nI"), xend(t - 1, 0, n), n)])],
+               ["I", "nI", "c240", "L" + p] + rx(t - 1, 0, n) + ["T%s%d_%d" % (k, s, c) for k in "la" for s in range(1, t)], B)
+            pe("R" + q, [(pa[:, r(0)], R), (pa[:, r(1)], R + [(M("nI"), X, n)])], rR + ["nI", "L" + p], A)
+            gs = [(pa[:, r(2)], [(M("nBk"), pl(T.kb, t - 1), n), kb])]
+            if last:
+                gs.append((pa[:, r(3)], [kb]))
+            pe("sig" + q, gs, ["Bk", "nBk", "kb" + q, "kb" + p], A)
+            if "sw" in PAR["scalar"]:
+                act("sw" + q, n, [], ["sw%d" % c], lambda pa=pa: S.activation(T.sw[:, cs], pa[:, r(2)], ACT.Abs, scale=1.0 / 2048), [A])
+            else:
+                vec("sw" + q, n, [], ["sw%d" % c], ts(T.sw[:, cs], pa[:, r(2)], 0.0, ALU.not_equal), [A])
+            vec("Tl" + q, n, ["sw%d" % c], ["Tl" + q], tt(pl(T.tl, t), pb[:, r(0)], T.sw[:, cs], ALU.mult), [B])
+            vec("eq" + q, n, ["Tl" + q], ["eq%d" % c], tt(T.eq[:, cs], pa[:, r(1)], pl(T.tl, t), ALU.is_equal), [A])
+            vec("Ta" + q, n, ["sw%d" % c], ["Ta" + q], tt(pl(T.ta, t), pb[:, r(1)], T.sw[:, cs], ALU.mult), [B])
+            eq = (M("nQ"), T.eq[:, cs], n)
+            pe2("offp" + q, [(po[:, 2 * n + 1:4 * n:2], R + [kb, eq]),
+                             (po[:, 2 * n:4 * n:2], [(M("I"), X, n), (M("Bk2"), pl(T.kb, t), n), (M("I"), pl(T.tl, t), n), eq])], 1,
+                rR + ["Bk", "Bk2", "kb" + q, "Tl" + q, "L" + p], ["nQ", "eq%d" % c], O)
+            vec("off" + q, 2 * n, [], ["off%d" % c], lambda: V.tensor_copy(T.off[:, o0:o0 + 2 * n], po[:, 2 * n:4 * n]), [O])
+        vec("L" + q, n, [], ["L" + q], ts(pl(T.lst, t), pa[:, r(0)], 0.0, ALU.max), [A])
+
+        def closing(kind, X, rX, buf, nm, outbuf, dram):
+            hist = [(M("nI"), pl(buf, s), n) for s in range(1, PLIES)]
+            rh = [nm + "%d_%d" % (s, c) for s in range(1, PLIES)]
+            cz = [(M("I"), c240, n)] if kind == "a" else []
+            up = [(M("nI"), c240, n)] if kind == "a" else []
+            f = nm + "f%d" % c
+            B = bank("end" if kind == "c" or PAR["banks"] == "chunk" else "ZR"[c % 2], c)
+            pb = T[B]
+            pe("Zf" + kind + q, [(pb[:, r(0)], hist + cz + [(M("nI"), X, n)])], rh + rX + ["nI", "I", "c240"], B)
+            vec(f, n, ["bb%d" % c], [f], tt(pl(buf, PLIES), pb[:, r(0)], T.bb[:, cs], ALU.mult), [B])
+            pe("Cf" + kind + q, [(pb[:, r(1)], up + [(M("I"), X, n), (M("I"), pl(buf, PLIES), n)]),
+                                 (pb[:, r(2)], hist + [(M("nI"), pl(buf, PLIES), n)])], rh + rX + [f, "nI", "I", "c240"], B)
+            for b in range(2):
+                act("o%s%d_%d" % (kind, b, c), n, [], ["o%s%d_%d" % (kind, b, c)],
+                    scaled(outbuf[:, o0 + b:o0 + 2 * n:2], pb[:, r(1 + b)], 1), [B])
+            add("S", "st" + kind + q, ("d", 2.0), ["o%s%d_%d" % (kind, b, c) for b in range(2)], [],
+                lambda: g.sync.dma_start(dram[:, o0:o0 + 2 * n], outbuf[:, o0:o0 + 2 * n]), token=("outs", 16 * 3 * nch))
+
+        if last:
+            vec("bb" + q, n, [], ["bb%d" % c], ts(T.bb[:, cs], pa[:, r(3)], 0.0, ALU.not_equal), [A])
+            closing("c", pl(T.lst, t), ["L" + q], T.tl, "Tl", T.oc, T.yc)
+
+        win = T.tab[:, 0:4096] if t == 0 else T.tab[:, 0:8192]
+        rt = ["tab"] + ([] if t == 0 else ["neg%d" % k for k in range(4)])
+        d = (t * nch + c) % ND1
+        f0 = 32 * CW * d
+        i = 0
+        D1 = bank("d1", c)
+        pd = T[D1]
+        for h, part in enumerate(pieces(n, *PAR["gat0" if t == 0 else "gat1"])):
+            i0 = i
+            for e, k in part:
+                j = i + k
+                src = T.off[:, o0 + i * w // 16:o0 + j * w // 16]
+                out = T.gw[:, g0 + i * w:g0 + j * w]
+                if e == "A":
+                    fn = lambda out=out, src=src: S.activation(out, win.indirect(src), ACT.Copy)
+                else:
+                    fn = lambda out=out, src=src: V.tensor_copy(out, win.indirect(src))
+                add(e, "gat%s_%d" % (q, i), ("gat", k * w), rt + ["off%d" % c], cols("gw%d" % c, i * w, j * w), fn)
+                i = j
+            m, qh = i - i0, "%s_%d" % (q, h)
+            rg, rf = cols("gw%d" % c, i0 * w, i * w), cols("flo%d" % d, i0 * 32, i * 32)
+            first = T.gw[:, g0 + i0 * w:g0 + i * w:w]
+            ffirst = T.flo[:, f0 + 32 * i0:f0 + 32 * i:32]
+            if t == 0:
+                vec("d1" + qh, m // 2, rg, rf, ts(ffirst, first, -240.0, ALU.add, -240.0, ALU.max))
+                floor = T.flo[:, f0 + 32 * i0:f0 + 32 * i:2]
+            else:
+                ta = T.ta[:, t * LN + c0 + i0:t * LN + c0 + i]
+                pe2("d1p" + qh, [(pd[:, i0:i], [(M("I"), xend(t - 1, i0, i), 64), (M("I"), ta, 64), (M("I"), first, 64)])], 1,
+                    ["I", "Ta" + q] + rx(t - 1, i0, i), rg, D1)
+                vec("d1" + qh, m, [], rf, ts(ffirst, pd[:, i0:i], -240.0, ALU.max), [D1])
+                floor = T.flo[:, f0 + 32 * i0:f0 + 32 * i]
+            if PAR["reset"] == "G":
+                gps("rst" + qh, m, [], rg, lambda first=first, m=m: g.iota(first, [[0, m]], -1024, 0, allow_small_or_imprecise_dtypes=True))
+            else:
+                vec("rst" + qh, m // 2, [], rg, lambda first=first: V.memset(first, -1024.0))
+            xo = T.x0[:, 16 * (c0 + i0):16 * (c0 + i)] if t == 0 else T.xs[:, g0 + 32 * i0:g0 + 32 * i]
+            vec("scan" + qh, w * m // 2, rg + rf, rx(t, i0, i),
+                lambda xo=xo, a=T.gw[:, g0 + i0 * w:g0 + i * w], floor=floor: V.tensor_tensor_scan(xo, a, floor, -240.0, ALU.add, ALU.max))
+        xnow, rxn = xend(t, 0, n), rx(t, 0, n)
+        y = T.yv[:, cs]
+        vec("y" + q, n // 2, rxn, ["y%d" % c], ts(y, xnow, 240.0, ALU.add, 127.0, ALU.min))
+        Sc, Mx, G, A = bank("sc", c), bank("mx", c), bank("G", c), bank("raw", c)
+        sc, mx, pg, pa = T[Sc], T[Mx], T[G], T[A]
+        pe2("scp" + q, [(sc[0:n, 0:128], [(Ep, M("nM"), 128), (y, M("U4"), 128)])], 1, [rE, "nM"], ["y%d" % c, "UV4"], Sc)
+        pe("vlp" + q, [(sc[64:64 + n, 0:128], [(y, M("V4"), 128)])], ["y%d" % c, "UV4", "shut" + Sc], Sc)
+        pm = T.pm[:, 128 * c:128 * c + 128]
+        vec("max" + q, 128, ["tie"], ["pm%d" % c],
+            lambda: V.tensor_tensor_scan(pm, T.tie[:], sc[:, 0:128], 0.0, ALU.add, ALU.max), [Sc])
+        pe("mxp" + q, [(mx[0:8, 128:192 + n], [(T.pm[:, 128 * c + 15:128 * c + 128:16], T.i32[:, 0:64 + n], 256 + 4 * n)])],
+           ["pm%d" % c, "i32"], Mx)
+        m0, rm = 128 * ((t * nch + c) % 2), "mxs%d" % ((t * nch + c) % 2)
+        if "mx" in PAR["scalar"]:
+            act("mx" + q, 64 + n, [], [rm], scaled(T.mxs[0:8, m0:m0 + 64 + n], mx[0:8, 128:192 + n], 1), [Mx])
+        else:
+            vec("mx" + q, 64 + n, [], [rm], lambda: V.tensor_copy(T.mxs[0:8, m0:m0 + 64 + n], mx[0:8, 128:192 + n]), [Mx])
+        gr = (pg[:, r(0)], [(M("nU4"), y, n), (M("pM"), Ep, n), (T.sel[0:9, :], T.mxs[0:9, m0:m0 + n], 4 * n)])
+        gd = [(M("nV4"), y, n), (T.sel[0:9, :], T.mxs[0:9, m0 + 64:m0 + 64 + n], 4 * n)]
+        r0, r1 = ["nUV4", "pM", "y%d" % c, rE], ["sel", rm]
+        if "sth" in PAR["scalar"]:
+            D = bank("G2", c)
+            gdo = T[D][:, r(3)]
+            pe2("Gr" + q, [gr], 1, r0, r1, G)
+            pe("Gd" + q, [(gdo, gd)], r0 + r1, D)
+        else:
+            D, gdo = G, pg[:, r(1)]
+            pe2("Gr" + q, [gr, (gdo, gd)], 1, r0, r1, G)
+        vec("b" + q, n, [rS], ["b" + q], tt(bp, pg[:, r(0)], Sp, ALU.min), [G])
+        sth = T.sth[:, cs]
+        if "sth" in PAR["scalar"]:
+            act("sth" + q, n, ["stf"], ["sth%d" % c],
+                lambda: S.activation(sth, gdo, ACT.Relu, bias=T.col[:, 2:3], scale=-1.0), [D])
+        else:
+            vec("sth" + q, n, ["stf"], ["sth%d" % c], ts(sth, gdo, 0.0, ALU.is_equal, T.col[:, 2:3], ALU.mult), [D])
+        js = (M("J"), sth, n)
+        pe2("raw" + q, [(pa[:, r(0)], [(M("J"), Sp, n), (M("nJ"), bp, n), js]),
+                        (pa[:, r(1)], [(M("JmI"), Sp, n), (M("nJ"), bp, n), js]),
+                        (pa[:, r(2)], [(M("J"), Sp, n), (M("nJ4"), bp, n), js])], 2,
+            ["J", "JmI", rS], ["nJ", "nJ4", "b" + q, "sth%d" % c], A)
+        wn = T.wn[:, cs]
+        vec("wn" + q, n, [], ["wn%d" % c], ts(wn, pa[:, r(0)], 256.0, ALU.is_ge, 128.0, ALU.mult), [A])
+        ob = 3 * c0
+        hit = T.outb[:, ob + n:ob + 2 * n]
+        mov = T.outb[:, ob + 2 * n:ob + 3 * n] if t % 2 == 0 else T.outb[:, ob:ob + n]
+        vec("mov" + q, n, ["wn%d" % c], ["mov%d" % c], tt(mov, pa[:, r(2)], wn, ALU.subtract), [A])
+        vec("hit" + q, n, ["wn%d" % c], ["hit%d" % c], tt(hit, pa[:, r(1)], wn, ALU.is_equal), [A])
+        if not last:
+            u = "%d_%d" % (t + 1, c)
+            lo, lo1, h = (t * LN + c0) * 3, ((t + 1) * LN + c0) * 3, n if t % 2 == 0 else 0
+
+            def onward():
+                tr = RemoteDMATransfer(dst_ids=[dst(1)], dma_engine_mask=wide, remote_sem=T.sem["arr" + u],
+                                       srcs=[T.outb[:, ob + h:ob + h + 2 * n], T.land[:, lo + h:lo + h + 2 * n]],
+                                       dst=T.land[:, lo1 + h:lo1 + h + 2 * n], alu_op=2)
+                return g.remote_dma_fused([tr], local_sem=T.sem["go%d" % c])
+            s = add("G", "snd" + q, ("r", 1), ["mov%d" % c, "hit%d" % c, "b" + q, rE], [], onward, token=("go%d" % c, ne * (t + 1)))
+            add("X", "arr" + u, ("x", 1), [], ["S" + u, "E" + u], None, token=("arr" + u, ne), after=s)
+        else:
+            later.append(((t, c, nch), lambda: closing("a", xnow, rxn, T.ta, "Ta", T.oa, T.ya)))
+            vec("snew" + q, 2 * n, ["mov%d" % c, "b" + q], ["snew%d" % c], tt(T.snew[:, cs], mov, bp, ALU.max))
+            pe("ylp" + q, [(pa[:, r(0)], [(M("I"), Kp, n), (M("nE"), Ep, n), (M("nE"), hit, n), (M("I"), T.snew[:, cs], n)])],
+               [rK, rE, "I", "nE", "hit%d" % c, "snew%d" % c], A)
+            act("yl" + q, n, [], ["ol%d" % c], lambda: S.activation(T.ol[:, cs], pa[:, r(0)], ACT.Relu), [A])
+            add("S", "stl" + q, ("d", 2.0), ["ol%d" % c], [], lambda: g.sync.dma_start(T.yl[:, cs], T.ol[:, cs]),
+                token=("outs", 16 * 3 * nch))
+
+    for t in range(PLIES):
+        for c in range(nch):
+            now[0] = (t, c, nch)
+            ply(t, c)
+    for at, fn in later:
+        now[0] = at
+        fn()
+    return ops
+
+
+def depend(ops):
+    wr, rd, run = {}, {}, {}
+    deps = []
+    for i, o in enumerate(ops):
+        d = set()
+        for x in o["r"]:
+            if x in wr:
+                d.add(wr[x])
+        for x in o["w"]:
+            if x in wr:
+                d.add(wr[x])
+            d.update(rd.get(x, []))
+        for b in o["banks"]:
+            e, cur, prev = run.get(b, (None, [], []))
+            if e == o["eng"]:
+                d.update(prev)
+                cur.append(i)
+            else:
+                d.update(cur)
+                run[b] = (o["eng"], [i], cur)
+        for x in o["r"]:
+            rd.setdefault(x, []).append(i)
+        for x in o["w"]:
+            wr[x] = i
+            rd[x] = []
+        d.discard(i)
+        deps.append(sorted(d))
+    return deps
+
+
+def waits(ops, i, j):
+    return not (ops[i]["eng"] == "P" and ops[j]["eng"] == "P")
+
+
+def times(o, par):
+    k, x = o["cost"]
+    if k == "v":
+        a = par["fix"] + x * par["cyc"]
+        return a, a
+    if k == "gat":
+        a = 0.06 + x * par["gat"] * par["cyc"]
+        return a, a
+    if k == "g":
+        a = 0.16 + 2 * x * par["cyc"]
+        return a, a
+    if k == "p":
+        return x * par["pe"], x * par["pe"] + par["pefix"]
+    if k == "d":
+        return 0.1, x
+    if k == "r":
+        return par["issue"], par["wire"]
+    return 0.0, par["wire"] * x
+
+
+def schedule(ops, deps, par):
+    m = len(ops)
+    tm = [times(o, par) for o in ops]
+    nxt = [[] for _ in ops]
+    for i in range(m):
+        for j in deps[i]:
+            nxt[j].append(i)
+    way = [0.0] * m
+    for i in range(m - 1, -1, -1):
+        t, c, nch = ops[i]["chunk"]
+        due = -(c * par["beat0"] if t == 0 else nch * par["beat0"] + ((t - 1) * nch + c) * par["beat"])
+        way[i] = max([way[j] + par["hop"] for j in nxt[i]] or [due]) + tm[i][1]
+        if ops[i]["name"].startswith("snd"):
+            way[i] = due + tm[i][1]
+        if ops[i]["name"] == "ksend":
+            way[i] = par["kway"]
+    rng = np.random.default_rng(par["seed"])
+    for i in range(m):
+        way[i] += float(rng.random()) * par["noise"] + par.get("bias", {}).get(i, 0.0)
+    done, left = [None] * m, [len(d) for d in deps]
+    ready = [0.0] * m
+    free = {e: 0.0 for e in "VAPGS"}
+    pool = {e: [i for i in range(m) if ops[i]["eng"] == e and not left[i]] for e in "VAPGS"}
+    arrive = {o["after"]: i for i, o in enumerate(ops) if o["after"] is not None}
+    order = []
+
+    def finish(i, begun, at):
+        done[i] = at
+        for j in nxt[i]:
+            ready[j] = max(ready[j], at + par["hop"] if waits(ops, j, i) else begun)
+            left[j] -= 1
+            if not left[j]:
+                pool[ops[j]["eng"]].append(j)
+    while any(pool.values()):
+        e = min((x for x in pool if pool[x]), key=lambda x: max(free[x], min(ready[i] for i in pool[x])))
+        now = max(free[e], min(ready[i] for i in pool[e]))
+        i = max((j for j in pool[e] if ready[j] <= now + par["look"]), key=lambda j: (way[j], -j))
+        pool[e].remove(i)
+        now = max(now, ready[i])
+        free[e] = now + tm[i][0]
+        order.append(i)
+        finish(i, now, now + tm[i][1])
+        if i in arrive:
+            order.append(arrive[i])
+            finish(arrive[i], now, now + tm[arrive[i]][1])
+    return order, max(done)
+
+
+PLAN = {}
+
+
+def rank_program(g, core, T, topo):
+    if T.rank_of(core) is None:
+        return
+    ops = build(g, T, core, topo)
+    if not PLAN:
+        PLAN["deps"] = depend(ops)
+        PLAN["order"] = schedule(ops, PLAN["deps"], PAR)[0]
+    deps = PLAN["deps"]
+    queue = {"V": g.vector, "A": g.scalar, "P": g.tensor, "G": g, "S": g.sync}
+    known = {e: {} for e in queue}
+    count = {e: 0 for e in queue}
+    token, clock, total = {}, {}, {}
+    for i in PLAN["order"]:
+        o = ops[i]
+        e = o["eng"]
+        if e == "X":
+            token[i] = o["token"]
+            clock[i] = {o["token"][0]: o["token"][1]}
+            total[o["token"][0]] = o["token"][1]
+            continue
+        kn = known[e]
+        for j in sorted(deps[i], key=lambda j: -token[j][1]):
+            s, v = token[j]
+            if kn.get(s, 0) < v and waits(ops, i, j):
+                queue[e].wait_ge(T.sem[s], v)
+                for a, b in clock[j].items():
+                    kn[a] = max(kn.get(a, 0), b)
+        ins = o["fn"]()
+        if o["token"] is None:
+            count[e] += 1
+            token[i] = ("c" + e, count[e])
+            ins.then_inc(T.sem["c" + e], 1)
+        else:
+            token[i] = o["token"]
+            if o["cost"][0] == "d":
+                ins.then_inc(T.sem[o["token"][0]], 16)
+        clock[i] = dict(kn)
+        clock[i][token[i][0]] = token[i][1]
+        total[token[i][0]] = max(total.get(token[i][0], 0), token[i][1])
+    seen = {}
+    for kn in known.values():
+        for a, b in kn.items():
+            seen[a] = max(seen.get(a, 0), b)
+    for s, v in total.items():
+        if seen.get(s, 0) < v:
+            g.sync.wait_ge(T.sem[s], v)

@@ -10,23 +10,24 @@ ND1 = 2
 PAR = {
     "widths": (64, 64, 64, 64),
     "banks": "stage",
-    "gat0": (0, 32, 32), "gat1": (4, 16, 40),
+    "gat0": (12, 0, 28), "gat1": (4, 24, 40),
+    "bias": {239:-1.1,658:-0.4,485:0.7,871:1.4,659:0.4,880:-1.0,868:3.0,777:-0.7,139:-1.4,55:-1.8,823:1.1,23:0.9,156:0.3,348:1.6,196:0.2,338:-1.6,399:0.2,228:0.7,803:-0.9,913:-1.9,733:2.1,256:0.8,305:1.3,564:2.0,388:-0.7,469:-0.5,36:0.5,561:-1.3,932:-1.0,477:-0.8,821:-3.7,533:0.8,151:1.7,26:-0.9,907:-0.4,304:-0.8,495:-0.3,462:0.7,647:-1.6,344:-0.4,459:1.0,301:-0.2,59:1.5,622:-1.4,870:0.1,499:-0.4,520:-1.3,404:1.5,205:-1.5,252:2.0,682:-0.4,743:-0.2,12:0.5,32:1.6,526:2.5,5:0.4,686:-0.6,60:-1.2,163:1.1,830:-1.8,730:-0.4,786:1.3,747:-0.9,128:-2.4,862:-0.3},
     "early": True,
     "negv": 1,
     "scalar": (),
     "reset": "G",
-    "hop": 0.10, "fix": 0.03, "cyc": 0.001, "gat": 1.56, "pe": 0.0005, "pefix": 0.08, "issue": 0.8, "wire": 2.6,
-    "beat0": 2.2, "beat": 2.6, "kway": 3.0, "look": 0.05, "seed": 0, "noise": 0.0,
+    "hop": 0.11, "fix": 0.05, "cyc": 0.001, "gat": 1.8, "pe": 0.00045, "pemm": 0.0, "pefix": 0.12, "issue": 0.8, "wire": 2.6,
+    "beat0": 2.2, "beat": 3.0, "kway": 3.0, "look": 0.05, "seed": 0, "noise": 0.0,
 }
-MATS = ["one", "I", "nI", "J", "nJ", "JmI", "nJ4", "Bk", "nBk", "Bk2", "nE", "nQ", "nM", "pM", "U1", "V1", "U4", "V4", "nU4", "nV4"]
+MATS = ["one", "I", "nI", "J", "nJ", "nJ1", "Bk", "nBk", "Bk2", "nE", "nQ", "nM", "I2", "nI2", "U1", "V1"]
 
 SCRATCH = {
     "tab": ("sbuf", [128, 8192], "bfloat16"),
     "posi": ("sbuf", [128, LN], "int32"), "sqi": ("sbuf", [128, LN], "int32"), "kni": ("sbuf", [128, LN], "int32"),
     "uv": ("sbuf", [128, 32], "bfloat16"), "sti": ("sbuf", [128, 8], "int32"), "col": ("sbuf", [128, 8], "float32"),
-    "pi": ("sbuf", [128, 16], "int32"), "pu": ("sbuf", [128, 8], "uint16"),
+    "pi": ("sbuf", [128, 24], "int32"), "pu": ("sbuf", [128, 16], "uint16"),
     "mat": ("sbuf", [128, 128 * len(MATS)], "bfloat16"),
-    "i32": ("sbuf", [128, 128], "float32"), "sel": ("sbuf", [128, 128], "float32"), "tie": ("sbuf", [128, 128], "float32"),
+    "nk": ("sbuf", [128, 128], "bfloat16"), "top": ("sbuf", [128, 288], "bfloat16"), "tie": ("sbuf", [128, 128], "float32"),
     "kin": ("sbuf", [128, PLIES * LN], "bfloat16"),
     "land": ("sbuf", [128, PLIES * 3 * LN], "bfloat16"), "outb": ("sbuf", [128, 3 * LN], "bfloat16"),
     "kb": ("sbuf", [128, PLIES * LN], "bfloat16"), "sw": ("sbuf", [128, LN], "bfloat16"), "bb": ("sbuf", [128, LN], "bfloat16"),
@@ -38,7 +39,7 @@ SCRATCH = {
     "gw": ("sbuf", [128, 32 * LN], "bfloat16"), "xs": ("sbuf", [128, 32 * LN], "bfloat16"),
     "x0": ("sbuf", [128, 16 * LN], "bfloat16"),
     "flo": ("sbuf", [128, ND1 * 32 * CW], "bfloat16"),
-    "pm": ("sbuf", [128, NCH * 128], "float32"), "mxs": ("sbuf", [128, NCH * 128], "float32"),
+    "pm": ("sbuf", [128, NCH * 128], "float32"), "pw": ("sbuf", [128, NCH * 128], "float32"),
     "ol": ("sbuf", [128, LN], "float32"), "oa": ("sbuf", [128, 2 * LN], "float32"), "oc": ("sbuf", [128, 2 * LN], "float32"),
 }
 for _c in range(8):
@@ -100,7 +101,7 @@ def build(g, T, core, topo):
                     s0, s1 = begin and k == 0, end and k == len(flat) - 1
                 last = P.matmul(out, a, b, s0, s1)
             return last
-        add("P", name, ("p", sum(x[2] for _, ts in groups for x in ts)), reads + ([] if begin else ["open" + bank]),
+        add("P", name, ("p", [x[2] for _, ts in groups for x in ts]), reads + ([] if begin else ["open" + bank]),
             ([] if end else ["open" + bank]) + ([] if begin else ["shut" + bank]), fn, [bank])
 
     def pe2(name, groups, k, reads0, reads1, bank):
@@ -137,35 +138,31 @@ def build(g, T, core, topo):
     gps("J0", 128, ["one"], ["J"], lambda: g.affine_select(M("J"), M("one"), blk, ALU.is_ge, 0.0, 0, 1))
     gps("J1", 128, ["J"], ["J"], lambda: g.affine_select(M("J"), M("J"), [[16, 8], [0, 16]], ALU.is_ge, 0.0, 15, -1))
     gps("pi", 8, [], ["pi"], lambda: g.iota(T.pi[:, 0:8], [[0, 8]], 0, 1))
-    gps("sel0", 128, [], ["sel"], lambda: g.iota(T.sel[0:32, :], [[0, 8], [256, 16]], -3840, 0, allow_small_or_imprecise_dtypes=True))
-    gps("sel1", 128, ["sel"], ["sel"], lambda: g.affine_select(T.sel[0:32, :], T.sel[0:32, :], [[0, 128]], ALU.is_ge, 0.0, -8, 1))
-    gps("sel2", 128, ["sel"], ["sel"], lambda: g.affine_select(T.sel[0:32, :], T.sel[0:32, :], [[-1, 8], [0, 16]], ALU.not_equal, 1.0, 0, 1))
-    gps("JmI0", 128, ["J"], ["JmI"], lambda: g.affine_select(M("JmI"), M("J"), dia, ALU.not_equal, 0.0, 0, 1))
-    gps("JmI1", 128, ["JmI"], ["JmI"], lambda: g.affine_select(M("JmI"), M("JmI"), [[-16, 8], [-1000, 16]], ALU.not_equal, 2.0, 0, 1))
+    gps("pe", 8, [], ["pe"], lambda: g.iota(T.pi[:, 16:24], [[1, 8]], 0, 0))
+    vec("pe16", 8, ["pe", "pu"], ["pe16"], lambda: V.tensor_copy(T.pu[:, 8:16], T.pi[:, 16:24]))
     act("nJ", 128, ["J"], ["nJ"], scaled(M("nJ"), M("J"), -1))
-    gps("nJ4", 128, ["nJ"], ["nJ4"], lambda: g.affine_select(M("nJ4"), M("nJ"), dia, ALU.not_equal, -5.0, 0, 1))
+    gps("nJ0", 128, ["nJ"], ["nJ1"], lambda: g.affine_select(M("nJ1"), M("nJ"), dia, ALU.not_equal, -2.0, 0, 1))
+    gps("nJ1", 128, ["nJ1"], ["nJ1"], lambda: g.affine_select(M("nJ1"), M("nJ1"), [[-16, 8], [-1000, 16]], ALU.not_equal, -3.0, 0, 1))
     gps("Bk2", 128, ["Bk"], ["Bk2"], lambda: g.affine_select(M("Bk2"), M("Bk"), blk, ALU.not_equal, 2.0, -1, 1))
-    for nm, k in (("nE", -4096), ("nI", -1), ("nQ", -16384), ("nM", -2.0 ** 31), ("pM", 2.0 ** 31)):
+    for nm, k in (("nE", -4096), ("nI", -1), ("nQ", -16384), ("nM", -2.0 ** 20), ("I2", 256), ("nI2", -256)):
         act(nm, 128, ["I"], [nm], scaled(M(nm), M("I"), k))
-    act("i32", 128, ["I"], ["i32"], scaled(T.i32[:], M("I"), 1))
+    vec("nk0", 64, [], ["nk"], lambda: V.memset(T.nk[:], 2.0))
+    vec("nk1", 8, ["nk"], ["nk"], lambda: V.memset(T.nk[:, 0:128:16], 0.0))
+    vec("top", 8, [], ["top0", "top1"], lambda: V.memset(T.top[:, 15:288:144], 1.0))
     act("nBk", 128, ["Bk"], ["nBk"], scaled(M("nBk"), M("Bk"), -1))
     vec("thr0", 128, ["Bk"], ["thr0"], lambda: V.tensor_reduce(T.col[:, 0:1], M("Bk"), AxisListType.X, ALU.add))
     vec("thr", 1, ["thr0"], ["thr"], ts(T.col[:, 1:2], T.col[:, 0:1], 12.0, ALU.mult))
+    vec("win", 1, ["thr0"], ["win"], ts(T.col[:, 3:4], T.col[:, 0:1], 0.0, ALU.mult))
     vec("stf", 1, ["sti"], ["stf"], lambda: V.tensor_copy(T.col[:, 2:3], T.sti[:, 0:1]))
     vec("pj", 8, ["pi"], ["pj"], ts(T.pi[:, 8:16], T.pi[:, 0:8], 15, ALU.bitwise_and))
-    vec("pu", 8, ["pj"], ["pu"], lambda: V.tensor_copy(T.pu[:], T.pi[:, 8:16]))
+    vec("pu", 8, ["pj"], ["pu"], lambda: V.tensor_copy(T.pu[:, 0:8], T.pi[:, 8:16]))
     vec("U1", 250, ["pu", "u", "J"], ["U1"], lambda: V.tensor_tensor(M("U1"), T.uv[:, 0:16].indirect(T.pu[:, 0:8]), M("J"), ALU.mult))
     vec("V1", 250, ["pu", "v", "J"], ["V1"], lambda: V.tensor_tensor(M("V1"), T.uv[:, 16:32].indirect(T.pu[:, 0:8]), M("J"), ALU.mult))
-    k1, k4, k5 = MATS.index("U1") * 128, MATS.index("U4") * 128, MATS.index("nU4") * 128
-    act("UV4", 256, ["U1", "V1"], ["UV4"], scaled(T.mat[:, k4:k4 + 256], T.mat[:, k1:k1 + 256], 4096))
-    act("nUV4", 256, ["U1", "V1"], ["nUV4"], scaled(T.mat[:, k5:k5 + 256], T.mat[:, k1:k1 + 256], -4096))
     for k in range(ND1):
         vec("flo%d" % k, 16 * n, [], cols("flo%d" % k, 0, 32 * n) + ([] if k else ["c240"]),
             lambda k=k: V.memset(T.flo[:, 32 * n * k:32 * n * (k + 1)], -240.0))
-    vec("tie0", 128, [], ["tie"], lambda: V.memset(T.tie[:], 256.0))
+    vec("tie0", 128, [], ["tie"], lambda: V.memset(T.tie[:], 0.0))
     vec("tie1", 8, ["tie"], ["tie"], lambda: V.memset(T.tie[:, 0:128:16], -2.0 ** 33))
-    gps("mxs", 128, [], ["mxs0"], lambda: g.iota(T.mxs[0:32, 0:128], [[0, 128]], 1, 0, allow_small_or_imprecise_dtypes=True))
-    gps("mxs", 128, [], ["mxs1"], lambda: g.iota(T.mxs[0:32, 128:256], [[0, 128]], 1, 0, allow_small_or_imprecise_dtypes=True))
     for b in sorted(set(bank("sc", c) for c in range(nch) if W[c] < 64)):
         vec("clr" + b, 128, [], [], lambda b=b: V.memset(T[b][:, 0:128], 0.0), [b])
 
@@ -250,7 +247,10 @@ def build(g, T, core, topo):
             pe("Z" + q, [(pb[:, r(0)], hl + [(M("nI"), X, n)]),
                          (pb[:, r(1)], ha + [(M("I"), c240, n), (M("nI"), xend(t - 1, 0, n), n)])],
                ["I", "nI", "c240", "L" + p] + rx(t - 1, 0, n) + ["T%s%d_%d" % (k, s, c) for k in "la" for s in range(1, t)], B)
-            pe("R" + q, [(pa[:, r(0)], R), (pa[:, r(1)], R + [(M("nI"), X, n)])], rR + ["nI", "L" + p], A)
+            pe("R" + q, [(pb[:, r(2)], R)], rR, B)
+            vec("L" + q, n, [], ["L" + q], ts(pl(T.lst, t), pb[:, r(2)], 0.0, ALU.max), [B])
+            Lt = (M("I"), pl(T.lst, t), n)
+            pe("RX" + q, [(pb[:, r(3)], [(M("nI"), X, n), Lt])], ["I", "nI", "L" + p, "L" + q], B)
             gs = [(pa[:, r(2)], [(M("nBk"), pl(T.kb, t - 1), n), kb])]
             if last:
                 gs.append((pa[:, r(3)], [kb]))
@@ -260,14 +260,15 @@ def build(g, T, core, topo):
             else:
                 vec("sw" + q, n, [], ["sw%d" % c], ts(T.sw[:, cs], pa[:, r(2)], 0.0, ALU.not_equal), [A])
             vec("Tl" + q, n, ["sw%d" % c], ["Tl" + q], tt(pl(T.tl, t), pb[:, r(0)], T.sw[:, cs], ALU.mult), [B])
-            vec("eq" + q, n, ["Tl" + q], ["eq%d" % c], tt(T.eq[:, cs], pa[:, r(1)], pl(T.tl, t), ALU.is_equal), [A])
+            vec("eq" + q, n, ["Tl" + q], ["eq%d" % c], tt(T.eq[:, cs], pb[:, r(3)], pl(T.tl, t), ALU.is_equal), [B])
             vec("Ta" + q, n, ["sw%d" % c], ["Ta" + q], tt(pl(T.ta, t), pb[:, r(1)], T.sw[:, cs], ALU.mult), [B])
             eq = (M("nQ"), T.eq[:, cs], n)
-            pe2("offp" + q, [(po[:, 2 * n + 1:4 * n:2], R + [kb, eq]),
+            pe2("offp" + q, [(po[:, 2 * n + 1:4 * n:2], [Lt, kb, eq]),
                              (po[:, 2 * n:4 * n:2], [(M("I"), X, n), (M("Bk2"), pl(T.kb, t), n), (M("I"), pl(T.tl, t), n), eq])], 1,
-                rR + ["Bk", "Bk2", "kb" + q, "Tl" + q, "L" + p], ["nQ", "eq%d" % c], O)
+                ["I", "Bk", "Bk2", "kb" + q, "Tl" + q, "L" + p, "L" + q], ["nQ", "eq%d" % c], O)
             vec("off" + q, 2 * n, [], ["off%d" % c], lambda: V.tensor_copy(T.off[:, o0:o0 + 2 * n], po[:, 2 * n:4 * n]), [O])
-        vec("L" + q, n, [], ["L" + q], ts(pl(T.lst, t), pa[:, r(0)], 0.0, ALU.max), [A])
+        if t == 0:
+            vec("L" + q, n, [], ["L" + q], ts(pl(T.lst, t), pa[:, r(0)], 0.0, ALU.max), [A])
 
         def closing(kind, X, rX, buf, nm, outbuf, dram):
             hist = [(M("nI"), pl(buf, s), n) for s in range(1, PLIES)]
@@ -333,49 +334,35 @@ def build(g, T, core, topo):
         xnow, rxn = xend(t, 0, n), rx(t, 0, n)
         y = T.yv[:, cs]
         vec("y" + q, n // 2, rxn, ["y%d" % c], ts(y, xnow, 240.0, ALU.add, 127.0, ALU.min))
-        Sc, Mx, G, A = bank("sc", c), bank("mx", c), bank("G", c), bank("raw", c)
-        sc, mx, pg, pa = T[Sc], T[Mx], T[G], T[A]
-        pe2("scp" + q, [(sc[0:n, 0:128], [(Ep, M("nM"), 128), (y, M("U4"), 128)])], 1, [rE, "nM"], ["y%d" % c, "UV4"], Sc)
-        pe("vlp" + q, [(sc[64:64 + n, 0:128], [(y, M("V4"), 128)])], ["y%d" % c, "UV4", "shut" + Sc], Sc)
+        Sc, G, A = bank("sc", c), bank("G", c), bank("raw", c)
+        sc, pg, pa = T[Sc], T[G], T[A]
+        pe2("scp" + q, [(sc[0:n, 0:128], [(Ep, M("nM"), 128), (y, M("U1"), 128)])], 1, [rE, "nM"], ["y%d" % c, "U1"], Sc)
+        pe("vlp" + q, [(sc[64:64 + n, 0:128], [(y, M("V1"), 128)])], ["y%d" % c, "V1", "shut" + Sc], Sc)
         pm = T.pm[:, 128 * c:128 * c + 128]
         vec("max" + q, 128, ["tie"], ["pm%d" % c],
             lambda: V.tensor_tensor_scan(pm, T.tie[:], sc[:, 0:128], 0.0, ALU.add, ALU.max), [Sc])
-        pe("mxp" + q, [(mx[0:8, 128:192 + n], [(T.pm[:, 128 * c + 15:128 * c + 128:16], T.i32[:, 0:64 + n], 256 + 4 * n)])],
-           ["pm%d" % c, "i32"], Mx)
-        m0, rm = 128 * ((t * nch + c) % 2), "mxs%d" % ((t * nch + c) % 2)
-        if "mx" in PAR["scalar"]:
-            act("mx" + q, 64 + n, [], [rm], scaled(T.mxs[0:8, m0:m0 + 64 + n], mx[0:8, 128:192 + n], 1), [Mx])
-        else:
-            vec("mx" + q, 64 + n, [], [rm], lambda: V.tensor_copy(T.mxs[0:8, m0:m0 + 64 + n], mx[0:8, 128:192 + n]), [Mx])
-        gr = (pg[:, r(0)], [(M("nU4"), y, n), (M("pM"), Ep, n), (T.sel[0:9, :], T.mxs[0:9, m0:m0 + n], 4 * n)])
-        gd = [(M("nV4"), y, n), (T.sel[0:9, :], T.mxs[0:9, m0 + 64:m0 + 64 + n], 4 * n)]
-        r0, r1 = ["nUV4", "pM", "y%d" % c, rE], ["sel", rm]
-        if "sth" in PAR["scalar"]:
-            D = bank("G2", c)
-            gdo = T[D][:, r(3)]
-            pe2("Gr" + q, [gr], 1, r0, r1, G)
-            pe("Gd" + q, [(gdo, gd)], r0 + r1, D)
-        else:
-            D, gdo = G, pg[:, r(1)]
-            pe2("Gr" + q, [gr, (gdo, gd)], 1, r0, r1, G)
+        pw = T.pw[:, 8 * c:8 * c + 8]
+        vec("maw" + q, 8, ["pm%d" % c], ["pw%d" % c], lambda: V.tensor_copy(pw, T.pm[:, 128 * c + 15:128 * c + 128:16]))
+        m0, rm = 144 * ((t * nch + c) % 2) + 16, "top%d" % ((t * nch + c) % 2)
+        add("V", "top" + q, ("gat", 128), ["pm%d" % c, "pw%d" % c, "pe16"], [rm],
+            lambda: V.tensor_tensor(T.top[:, m0:m0 + 128], pw.indirect(T.pu[:, 8:16]), pm, ALU.is_equal))
+        k1 = 128 * MATS.index("one")
+        pe("Gre" + q, [(pg[:, 0:128], [(T.nk[:], T.mat[:, k1:k1 + 128], 128)])], ["nk", "one"], G, True, False)
+        pe("Gr" + q, [(pg[:, 0:128], [(T.top[:, m0 - 1:m0 + 127], M("I2"), 128), (T.top[:, m0:m0 + 128], M("nI2"), 128)])],
+           [rm, "I2", "nI2"], G, False, True)
         vec("b" + q, n, [rS], ["b" + q], tt(bp, pg[:, r(0)], Sp, ALU.min), [G])
         sth = T.sth[:, cs]
-        if "sth" in PAR["scalar"]:
-            act("sth" + q, n, ["stf"], ["sth%d" % c],
-                lambda: S.activation(sth, gdo, ACT.Relu, bias=T.col[:, 2:3], scale=-1.0), [D])
-        else:
-            vec("sth" + q, n, ["stf"], ["sth%d" % c], ts(sth, gdo, 0.0, ALU.is_equal, T.col[:, 2:3], ALU.mult), [D])
+        vec("sth" + q, n, ["stf", "win"], ["sth%d" % c], ts(sth, pg[:, 64:64 + n], T.col[:, 3:4], ALU.is_equal, T.col[:, 2:3], ALU.mult), [G])
         js = (M("J"), sth, n)
         pe2("raw" + q, [(pa[:, r(0)], [(M("J"), Sp, n), (M("nJ"), bp, n), js]),
-                        (pa[:, r(1)], [(M("JmI"), Sp, n), (M("nJ"), bp, n), js]),
-                        (pa[:, r(2)], [(M("J"), Sp, n), (M("nJ4"), bp, n), js])], 2,
-            ["J", "JmI", rS], ["nJ", "nJ4", "b" + q, "sth%d" % c], A)
+                        (pa[:, r(1)], [(M("J"), Sp, n), (M("nJ1"), bp, n), js])], 2,
+            ["J", rS], ["nJ", "nJ1", "b" + q, "sth%d" % c], A)
         wn = T.wn[:, cs]
         vec("wn" + q, n, [], ["wn%d" % c], ts(wn, pa[:, r(0)], 256.0, ALU.is_ge, 128.0, ALU.mult), [A])
         ob = 3 * c0
         hit = T.outb[:, ob + n:ob + 2 * n]
         mov = T.outb[:, ob + 2 * n:ob + 3 * n] if t % 2 == 0 else T.outb[:, ob:ob + n]
-        vec("mov" + q, n, ["wn%d" % c], ["mov%d" % c], tt(mov, pa[:, r(2)], wn, ALU.subtract), [A])
+        vec("mov" + q, n, ["wn%d" % c], ["mov%d" % c], tt(mov, pa[:, r(1)], wn, ALU.subtract), [A])
         vec("hit" + q, n, ["wn%d" % c], ["hit%d" % c], tt(hit, pa[:, r(1)], wn, ALU.is_equal), [A])
         if not last:
             u = "%d_%d" % (t + 1, c)
@@ -453,7 +440,8 @@ def times(o, par):
         a = 0.16 + 2 * x * par["cyc"]
         return a, a
     if k == "p":
-        return x * par["pe"], x * par["pe"] + par["pefix"]
+        a = sum(x) * par["pe"] + len(x) * par["pemm"]
+        return a, a + par["pefix"]
     if k == "d":
         return 0.1, x
     if k == "r":

@@ -1,3 +1,4 @@
+import math
 import numpy as np
 from concourse.bass import DstId, RemoteDMATransfer
 from concourse.mybir import AluOpType, AxisListType, ActivationFunctionType
@@ -5,53 +6,47 @@ from concourse.mybir import AluOpType, AxisListType, ActivationFunctionType
 ALU = AluOpType
 ACT = ActivationFunctionType
 N, LN, PLIES = 8, 256, 5
-NCH, CW = 8, 64
+NCH, CW = 4, 64
 ND1 = 2
+BIG = 2.0 ** 40
+MAGIC = 1.5 * 2.0 ** 30
+PEN = 2.0 ** 23
+DW = 136
 PAR = {
-    "widths": (64, 64, 64, 64),
-    "banks": "stage",
-    "gat0": (12, 0, 28), "gat1": (4, 24, 40),
-    "bias": {239:-1.1,658:-0.4,485:0.7,871:1.4,659:0.4,880:-1.0,868:3.0,777:-0.7,139:-1.4,55:-1.8,823:1.1,23:0.9,156:0.3,348:1.6,196:0.2,338:-1.6,399:0.2,228:0.7,803:-0.9,913:-1.9,733:2.1,256:0.8,305:1.3,564:2.0,388:-0.7,469:-0.5,36:0.5,561:-1.3,932:-1.0,477:-0.8,821:-3.7,533:0.8,151:1.7,26:-0.9,907:-0.4,304:-0.8,495:-0.3,462:0.7,647:-1.6,344:-0.4,459:1.0,301:-0.2,59:1.5,622:-1.4,870:0.1,499:-0.4,520:-1.3,404:1.5,205:-1.5,252:2.0,682:-0.4,743:-0.2,12:0.5,32:1.6,526:2.5,5:0.4,686:-0.6,60:-1.2,163:1.1,830:-1.8,730:-0.4,786:1.3,747:-0.9,128:-2.4,862:-0.3},
-    "early": True,
-    "negv": 1,
-    "scalar": (),
-    "reset": "G",
-    "hop": 0.11, "fix": 0.05, "cyc": 0.001, "gat": 1.8, "pe": 0.00045, "pemm": 0.0, "pefix": 0.12, "issue": 0.8, "wire": 2.6,
-    "beat0": 2.2, "beat": 3.0, "kway": 3.0, "look": 0.05, "seed": 0, "noise": 0.0,
+    "gat0": (0, 0, 64), "gat1": (16, 0, 64), "gat2": (0, 0, 64),
+    "gat0_0_1": (32, 0, 64), "gat1_0_0": (32, 0, 64), "gat4_3_1": (16, 0, 64),
+    "run": (32, 32),
+    "reset": "VV",
+    "keep": {"c": (2, 3, 4), "a": (3, 4)},
+    "hop": 0.15, "fix": 0.0, "cyc": 0.00104, "gat": 1.56, "pe": 0.0005, "pefix": 0.12, "issue": 0.8, "wire": 2.0,
+    "beat0": 2.2, "beat": 3.2, "kway": 3.0, "look": 0.0, "passes": 3, "tries": 22000, "warm": 0.04, "seed": 0,
 }
-MATS = ["one", "I", "nI", "J", "nJ", "nJ1", "Bk", "nBk", "Bk2", "nE", "nQ", "nM", "I2", "nI2", "U1", "V1"]
+COSTS = [(2.0, {"pe": 0.00048}),
+         (1.0, {"cyc": 0.00095, "gat": 1.3, "pe": 0.0008, "hop": 0.13, "wire": 2.1}),
+         (0.7, {"cyc": 0.0009, "gat": 1.5, "pe": 0.00045, "hop": 0.1, "issue": 1.0, "wire": 3.0})]
+MATS = ["one", "I", "nI", "J", "nJ", "nJ1", "Bk", "B", "IK", "nE", "nQ", "I2", "IP", "U1", "V1", "UT", "VT", "Th",
+        "JB", "nJB", "Same", "nSame", "Diff", "nDiff", "K0", "nK0", "K1", "nK1", "MG", "nMG", "IB", "nIB"]
 
 SCRATCH = {
-    "tab": ("sbuf", [128, 8192], "bfloat16"),
+    "tab": ("sbuf", [128, 4096], "bfloat16"),
     "posi": ("sbuf", [128, LN], "int32"), "sqi": ("sbuf", [128, LN], "int32"), "kni": ("sbuf", [128, LN], "int32"),
-    "uv": ("sbuf", [128, 32], "bfloat16"), "sti": ("sbuf", [128, 8], "int32"), "col": ("sbuf", [128, 8], "float32"),
-    "pi": ("sbuf", [128, 24], "int32"), "pu": ("sbuf", [128, 16], "uint16"),
+    "uv": ("sbuf", [128, 32], "bfloat16"), "sti": ("sbuf", [128, 8], "int32"), "col": ("sbuf", [128, 16], "float32"),
+    "pi": ("sbuf", [128, 16], "int32"), "pu": ("sbuf", [128, 8], "uint16"), "oh": ("sbuf", [128, 32], "float32"),
     "mat": ("sbuf", [128, 128 * len(MATS)], "bfloat16"),
-    "nk": ("sbuf", [128, 128], "bfloat16"), "top": ("sbuf", [128, 288], "bfloat16"), "tie": ("sbuf", [128, 128], "float32"),
+    "dm": ("sbuf", [128, 5 * 272], "bfloat16"), "rb": ("sbuf", [128, 256], "float32"), "ra": ("sbuf", [128, 256], "float32"), "zz": ("sbuf", [128, 256], "bfloat16"),
     "kin": ("sbuf", [128, PLIES * LN], "bfloat16"),
     "land": ("sbuf", [128, PLIES * 3 * LN], "bfloat16"), "outb": ("sbuf", [128, 3 * LN], "bfloat16"),
-    "kb": ("sbuf", [128, PLIES * LN], "bfloat16"), "sw": ("sbuf", [128, LN], "bfloat16"), "bb": ("sbuf", [128, LN], "bfloat16"),
-    "eq": ("sbuf", [128, LN], "bfloat16"), "yv": ("sbuf", [128, LN], "bfloat16"), "sth": ("sbuf", [128, LN], "bfloat16"),
-    "wn": ("sbuf", [128, LN], "bfloat16"), "snew": ("sbuf", [128, LN], "bfloat16"),
-    "lst": ("sbuf", [128, PLIES * LN], "float16"), "tl": ("sbuf", [128, (PLIES + 1) * LN], "float16"),
-    "ta": ("sbuf", [128, (PLIES + 1) * LN], "float16"),
+    "hh": ("sbuf", [128, PLIES * LN], "bfloat16"), "eq": ("sbuf", [128, LN], "bfloat16"), "yv": ("sbuf", [128, LN], "bfloat16"),
+    "sth": ("sbuf", [128, LN], "float16"), "lst": ("sbuf", [128, PLIES * LN], "float16"), "zs": ("sbuf", [128, 2 * PLIES * LN], "float16"),
     "off": ("sbuf", [128, 2 * LN], "uint16"),
-    "gw": ("sbuf", [128, 32 * LN], "bfloat16"), "xs": ("sbuf", [128, 32 * LN], "bfloat16"),
-    "x0": ("sbuf", [128, 16 * LN], "bfloat16"),
-    "flo": ("sbuf", [128, ND1 * 32 * CW], "bfloat16"),
-    "pm": ("sbuf", [128, NCH * 128], "float32"), "pw": ("sbuf", [128, NCH * 128], "float32"),
+    "gw": ("sbuf", [128, 32 * LN], "bfloat16"), "xs": ("sbuf", [128, (PLIES + 1) * 16 * LN], "float16"),
+    "flo": ("sbuf", [128, ND1 * 16 * CW], "float16"),
     "ol": ("sbuf", [128, LN], "float32"), "oa": ("sbuf", [128, 2 * LN], "float32"), "oc": ("sbuf", [128, 2 * LN], "float32"),
 }
 for _c in range(8):
     SCRATCH["ps%d" % _c] = ("psum", [128, 512], "float32")
-SEMAPHORES = (["cV", "cA", "cP", "cG", "ldp", "ldw", "ldf", "outs", "karr", "kgo"] + ["go%d" % c for c in range(NCH)]
+SEMAPHORES = (["cV", "cA", "cP", "cG", "ldp", "ldw", "ldf", "flo", "outs", "karr", "kgo"] + ["go%d" % c for c in range(NCH)]
               + ["arr%d_%d" % (t, c) for t in range(1, PLIES) for c in range(NCH)])
-STAGE = {"R": 0, "Z": 1, "off": 2, "d1": 3, "sc": 4, "mx": 4, "G": 5, "raw": 6, "yl": 6, "G2": 7, "end": 7}
-SECOND = ("Z", "off", "sc", "G", "end")
-
-
-def bank(stage, c):
-    return "ps%d" % (STAGE[stage] if PAR["banks"] == "stage" else 2 * c + (stage in SECOND))
 
 
 def pieces(n, v, tail, most):
@@ -67,21 +62,26 @@ def pieces(n, v, tail, most):
 def build(g, T, core, topo):
     rank = T.rank_of(core)
     ops = []
-    now = [(0, 0, 1)]
+    now = [(0, 0)]
     n = CW
-    W = PAR["widths"]
-    nch = len(W)
-    C0 = [sum(W[:c]) for c in range(nch)]
     V, S, P = g.vector, g.scalar, g.tensor
 
     def add(eng, name, cost, reads, writes, fn, banks=(), token=None, after=None):
         ops.append({"eng": eng, "name": name, "cost": cost, "r": list(reads), "w": list(writes), "fn": fn,
-                    "banks": list(banks), "token": token, "after": after, "chunk": now[0]})
+                    "banks": list(banks), "token": token, "after": after, "chunk": now[0], "ply": len(now) > 1,
+                    "kind": name.replace("%d_%d" % now[0], ":").replace(":_", "").split("_")[0].replace(":", "")})
         return len(ops) - 1
 
     def M(name):
         k = MATS.index(name)
         return T.mat[:, 128 * k:128 * k + 128]
+
+    def Mc(name, a, b, s=1):
+        k = 128 * MATS.index(name)
+        return T.mat[:, k + a:k + b:s]
+
+    def D(k, a=0, b=DW, s=1):
+        return T.dm[:, 272 * k + a:272 * k + b:s]
 
     def vec(name, cyc, reads, writes, fn, banks=()):
         add("V", name, ("v", max(64, cyc)), reads, writes, fn, banks)
@@ -92,23 +92,13 @@ def build(g, T, core, topo):
     def gps(name, cyc, reads, writes, fn):
         add("G", name, ("g", cyc), reads, writes, fn)
 
-    def pe(name, groups, reads, bank, begin=True, end=True):
+    def pe(name, terms, reads, bank, begin=False, end=True, cyc=n):
         def fn():
             last = None
-            flat = [(out, a, b, k == 0, k == len(terms) - 1) for out, terms in groups for k, (a, b, _) in enumerate(terms)]
-            for k, (out, a, b, s0, s1) in enumerate(flat):
-                if PAR["early"]:
-                    s0, s1 = begin and k == 0, end and k == len(flat) - 1
-                last = P.matmul(out, a, b, s0, s1)
+            for k, (out, a, b) in enumerate(terms):
+                last = P.matmul(out, a, b, begin and k == 0, end and k >= len(terms) - end)
             return last
-        add("P", name, ("p", [x[2] for _, ts in groups for x in ts]), reads + ([] if begin else ["open" + bank]),
-            ([] if end else ["open" + bank]) + ([] if begin else ["shut" + bank]), fn, [bank])
-
-    def pe2(name, groups, k, reads0, reads1, bank):
-        if not PAR["early"]:
-            return pe(name, groups, reads0 + reads1, bank)
-        pe(name + "e", [(o, ts[:-k]) for o, ts in groups], reads0, bank, True, False)
-        pe(name, [(o, ts[-k:]) for o, ts in groups], reads1, bank, False, True)
+        add("P", name, ("p", cyc * len(terms)), reads + ["acc" + bank], ["acc" + bank], fn, [bank])
 
     def ts(out, in0, s1, op0, s2=None, op1=None):
         if op1 is None:
@@ -119,12 +109,27 @@ def build(g, T, core, topo):
         return lambda: V.tensor_tensor(out, a, b, op)
 
     def scaled(out, in_, k):
-        return lambda: S.activation(out, in_, ACT.Copy, scale=float(k))
+        return lambda: S.activation(out, in_, ACT.Copy, scale=k)
+
+    def fill(out, k):
+        return lambda: V.memset(out, k)
+
+    def put(out, pattern, value, base):
+        return lambda: g.affine_select(out, out, pattern, ALU.not_equal, value, base, 1)
 
     def cols(name, a, b):
         return ["%s:%d" % (name, k) for k in range(a // 64, (b + 63) // 64)]
 
-    add("S", "ldf", ("d", 5.0), [], ["tab"], lambda: g.sync.dma_start(T.tab[:, 0:4096], T.feat[:]), token=("ldf", 16))
+    def col(k):
+        return T.col[:, k:k + 1]
+
+    def oh(k):
+        return T.oh[:, 16 + k:17 + k]
+
+    for b in range(2):
+        add("S", "ldf%d" % b, ("d", 4.8 - 0.1 * b), [], ["tab%d" % b],
+            lambda o=2048 * b: g.sync.dma_start(T.tab[:, o + 128:o + 2048], T.feat[:, o + 128:o + 2048]), token=("ldf", 32))
+        vec("tab%d" % b, 64, [], ["none%d" % b], fill(T.tab[:, 2048 * b:2048 * b + 128], 0.0))
     add("A", "ldp", ("d", 2.0), [], ["posi"], lambda: S.dma_start(T.posi[:], T.pos[:]), token=("ldp", 16))
     add("S", "ldu", ("d", 2.0), [], ["u"], lambda: g.sync.dma_start(T.uv[:, 0:16], T.u[:]), token=("ldw", 48))
     add("S", "ldv", ("d", 2.0), [], ["v"], lambda: g.sync.dma_start(T.uv[:, 16:32], T.v[:]), token=("ldw", 48))
@@ -132,51 +137,78 @@ def build(g, T, core, topo):
 
     blk = [[-16, 8], [0, 16]]
     dia = [[-1, 128]]
-    vec("one", 64, [], ["one"], lambda: V.memset(M("one"), 1.0))
+    vec("one", 64, [], ["one"], fill(M("one"), 1.0))
     gps("I", 128, ["one"], ["I"], lambda: g.affine_select(M("I"), M("one"), dia, ALU.is_equal, 0.0, 0, 1))
     gps("Bk", 128, ["one"], ["Bk"], lambda: g.affine_select(M("Bk"), M("one"), blk, ALU.is_equal, 0.0, 0, 1))
     gps("J0", 128, ["one"], ["J"], lambda: g.affine_select(M("J"), M("one"), blk, ALU.is_ge, 0.0, 0, 1))
     gps("J1", 128, ["J"], ["J"], lambda: g.affine_select(M("J"), M("J"), [[16, 8], [0, 16]], ALU.is_ge, 0.0, 15, -1))
     gps("pi", 8, [], ["pi"], lambda: g.iota(T.pi[:, 0:8], [[0, 8]], 0, 1))
-    gps("pe", 8, [], ["pe"], lambda: g.iota(T.pi[:, 16:24], [[1, 8]], 0, 0))
-    vec("pe16", 8, ["pe", "pu"], ["pe16"], lambda: V.tensor_copy(T.pu[:, 8:16], T.pi[:, 16:24]))
-    act("nJ", 128, ["J"], ["nJ"], scaled(M("nJ"), M("J"), -1))
-    gps("nJ0", 128, ["nJ"], ["nJ1"], lambda: g.affine_select(M("nJ1"), M("nJ"), dia, ALU.not_equal, -2.0, 0, 1))
-    gps("nJ1", 128, ["nJ1"], ["nJ1"], lambda: g.affine_select(M("nJ1"), M("nJ1"), [[-16, 8], [-1000, 16]], ALU.not_equal, -3.0, 0, 1))
-    gps("Bk2", 128, ["Bk"], ["Bk2"], lambda: g.affine_select(M("Bk2"), M("Bk"), blk, ALU.not_equal, 2.0, -1, 1))
-    for nm, k in (("nE", -4096), ("nI", -1), ("nQ", -16384), ("nM", -2.0 ** 20), ("I2", 256), ("nI2", -256)):
-        act(nm, 128, ["I"], [nm], scaled(M(nm), M("I"), k))
-    vec("nk0", 64, [], ["nk"], lambda: V.memset(T.nk[:], 2.0))
-    vec("nk1", 8, ["nk"], ["nk"], lambda: V.memset(T.nk[:, 0:128:16], 0.0))
-    vec("top", 8, [], ["top0", "top1"], lambda: V.memset(T.top[:, 15:288:144], 1.0))
-    act("nBk", 128, ["Bk"], ["nBk"], scaled(M("nBk"), M("Bk"), -1))
-    vec("thr0", 128, ["Bk"], ["thr0"], lambda: V.tensor_reduce(T.col[:, 0:1], M("Bk"), AxisListType.X, ALU.add))
-    vec("thr", 1, ["thr0"], ["thr"], ts(T.col[:, 1:2], T.col[:, 0:1], 12.0, ALU.mult))
-    vec("win", 1, ["thr0"], ["win"], ts(T.col[:, 3:4], T.col[:, 0:1], 0.0, ALU.mult))
-    vec("stf", 1, ["sti"], ["stf"], lambda: V.tensor_copy(T.col[:, 2:3], T.sti[:, 0:1]))
+    gps("rows", 16, [], ["rows"], lambda: g.iota(T.oh[:, 0:16], [[1, 16]], 0, 0, allow_small_or_imprecise_dtypes=True))
+    act("nJ", 128, ["J"], ["nJ"], scaled(M("nJ"), M("J"), -1.0))
+    act("nJ1", 128, ["J"], ["nJ1"], scaled(M("nJ1"), M("J"), -1.0))
+    gps("nJ2", 128, ["nJ1"], ["nJ1"], put(M("nJ1"), dia, -2.0, 0))
+    gps("nJ3", 128, ["nJ1"], ["nJ1"], put(M("nJ1"), [[-16, 8], [-1000, 16]], -3.0, 0))
+    for nm, src, k in (("B", "Bk", 2048.0), ("IP", "I", PEN), ("I2", "I", 256.0), ("MG", "I", MAGIC),
+                       ("nMG", "I", -MAGIC), ("nI", "I", -1.0), ("nQ", "I", -16384.0), ("JB", "J", BIG), ("nJB", "J", -BIG),
+                       ("K1", "Bk", BIG), ("nK1", "Bk", -BIG), ("IB", "I", BIG), ("nIB", "I", -BIG)):
+        act(nm, 128, [src], [nm], scaled(M(nm), M(src), k))
     vec("pj", 8, ["pi"], ["pj"], ts(T.pi[:, 8:16], T.pi[:, 0:8], 15, ALU.bitwise_and))
     vec("pu", 8, ["pj"], ["pu"], lambda: V.tensor_copy(T.pu[:, 0:8], T.pi[:, 8:16]))
-    vec("U1", 250, ["pu", "u", "J"], ["U1"], lambda: V.tensor_tensor(M("U1"), T.uv[:, 0:16].indirect(T.pu[:, 0:8]), M("J"), ALU.mult))
-    vec("V1", 250, ["pu", "v", "J"], ["V1"], lambda: V.tensor_tensor(M("V1"), T.uv[:, 16:32].indirect(T.pu[:, 0:8]), M("J"), ALU.mult))
-    for k in range(ND1):
-        vec("flo%d" % k, 16 * n, [], cols("flo%d" % k, 0, 32 * n) + ([] if k else ["c240"]),
-            lambda k=k: V.memset(T.flo[:, 32 * n * k:32 * n * (k + 1)], -240.0))
-    vec("tie0", 128, [], ["tie"], lambda: V.memset(T.tie[:], 0.0))
-    vec("tie1", 8, ["tie"], ["tie"], lambda: V.memset(T.tie[:, 0:128:16], -2.0 ** 33))
-    for b in sorted(set(bank("sc", c) for c in range(nch) if W[c] < 64)):
-        vec("clr" + b, 128, [], [], lambda b=b: V.memset(T[b][:, 0:128], 0.0), [b])
+    vec("pf", 1, ["pj"], ["pf"], lambda: V.tensor_copy(col(0), T.pi[:, 8:9]))
+    vec("oh", 16, ["pf", "rows"], ["oh"], ts(T.oh[:, 16:32], T.oh[:, 0:16], col(0), ALU.is_equal))
+    vec("thr", 1, ["oh"], ["thr"], ts(col(1), oh(0), 192.0, ALU.mult))
+    vec("win", 1, ["oh"], ["win"], ts(col(3), oh(0), 0.0, ALU.mult))
+    vec("stf", 1, ["sti"], ["stf"], ts(col(2), T.sti[:, 0:1], 64.5, ALU.add))
+    vec("cSame", 1, ["oh"], ["cSame"], ts(col(4), oh(0), oh(1), ALU.add, oh(15), ALU.subtract))
+    vec("cDiff", 1, ["oh"], ["cDiff"], ts(col(5), oh(0), oh(1), ALU.subtract))
+    vec("cK0", 1, ["oh"], ["cK0"], ts(col(6), oh(15), oh(0), ALU.subtract))
+    vec("cE", 1, ["oh"], ["cE"], ts(col(7), oh(0), 4096.0, ALU.mult))
+    vec("cnE", 1, ["oh"], ["cnE"], ts(col(8), oh(0), 4096.0, ALU.mult, -4096.0, ALU.add))
+    act("nE", 128, ["I", "cnE"], ["nE"], scaled(M("nE"), M("I"), col(8)))
+    act("IK", 128, ["I", "oh"], ["IK"], scaled(M("IK"), M("I"), oh(0)))
+    for nm, k in (("Same", 4), ("Diff", 5), ("K0", 6)):
+        act(nm, 128, ["JB", "c" + nm], [nm], scaled(M(nm), M("JB"), col(k)))
+        act("n" + nm, 128, ["nJB", "c" + nm], ["n" + nm], scaled(M("n" + nm), M("nJB"), col(k)))
+    vec("Th0", 64, [], ["Th"], fill(M("Th"), 0.0))
+    vec("Th1", 8, ["Th", "J", "oh"], ["Th1"], ts(Mc("Th", 0, 128, 16), Mc("J", 0, 128, 16), oh(15), ALU.mult, 192.0, ALU.mult))
+    vec("Th2", 8, ["Th", "J", "cK0"], ["Th2"], ts(Mc("Th", 1, 128, 16), Mc("J", 1, 128, 16), col(6), ALU.mult, 512.0, ALU.mult))
+    vec("D0", 16, ["IP"], ["DA"], tt(D(0, 128, 136), Mc("IP", 0, 128, 16), Mc("IP", 15, 128, 16), ALU.subtract))
+    vec("D6", 254, ["IP"], ["DB"], tt(D(0, 1, 128), Mc("IP", 1, 128), Mc("IP", 0, 127), ALU.subtract))
+    vec("D7", 8, ["DB"], ["DB"], fill(D(0, 0, 128, 16), 0.0))
+    for k, nm in enumerate("UV"):
+        b = "ps%d" % (3 + k)
+        add("V", nm + "1", ("gat", 128), ["pu", nm.lower(), "J"], [nm + "1"],
+            tt(M(nm + "1"), T.uv[:, 16 * k:16 * k + 16].indirect(T.pu[:, 0:8]), M("J"), ALU.mult))
+        vec(nm + "T", 64, [nm + "1"], [nm + "T"], lambda nm=nm: V.transpose(M(nm + "T"), M(nm + "1")))
+        pe(nm + "dp", [(T[b][:, 0:DW], M(nm + "T"), D(0))], [nm + "T", "DA", "DB"], b, True, True, DW)
+        act(nm + "d", DW, [], [nm + "d"], scaled(D(1 + k), T[b][:, 0:DW], -16.0 / PEN), [b])
+    act("C0", 128, ["J"], ["C"], scaled(D(3, 0, 128), M("J"), -4096.0))
+    act("C1", 8, ["J", "C"], ["C1"], scaled(D(3, 0, 128, 16), Mc("J", 0, 128, 16), 2.0 ** 42))
+    act("C2", 8, ["J"], ["C2"], scaled(D(3, 128, DW), Mc("J", 0, 128, 16), 15 * 4096.0))
+    pe("Cp", [(T.ps5[:, 0:DW], M("nE"), D(0)), (T.ps5[:, 0:DW], M("IK"), D(3))], ["nE", "IK", "DA", "DB", "C1", "C2"], "ps5", True, True, DW)
+    act("C", DW, ["C1", "C2"], ["C"], scaled(D(3), T.ps5[:, 0:DW], -1.0 / 4096), ["ps5"])
+    vec("zer", 68, [], ["zer"], fill(D(4, 0, 136), 0.0))
+    for k in range(2):
+        vec("rb%d" % k, 128, [], ["rb%d" % k], fill(T.rb[:, 128 * k:128 * k + 128], 0.0))
+    vec("flo0", 8 * n, [], cols("flo0", 0, 16 * n), fill(T.flo[:, 0:16 * n], 0.0))
+    for k in range(1, ND1):
+        add("S", "flo%d" % k, ("d", 2.5), cols("flo0", 0, 16 * n), cols("flo%d" % k, 0, 16 * n),
+            lambda k=k: g.sync.dma_start(T.flo[:, 16 * n * k:16 * n * (k + 1)], T.flo[:, 0:16 * n]), token=("flo", 16 * (ND1 - 1)))
 
     def land(t, c, what):
-        o, n = (t * LN + C0[c]) * 3, W[c]
+        o = (t * LN + c * n) * 3
         k = {"S": 0 if t % 2 == 0 else 2, "E": 1, "b": 2 if t % 2 == 0 else 0}[what]
         return T.land[:, o + k * n:o + (k + 1) * n]
 
     vec("sqi", LN, ["posi"], ["sqi"], ts(T.sqi[:], T.posi[:], 127, ALU.bitwise_and))
     vec("kni", LN, ["posi"], ["kni"], ts(T.kni[:], T.posi[:], 1920, ALU.bitwise_and))
-    vec("K0", LN, ["kni"], ["K0"], ts(T.kin[:, 0:LN], T.kni[:], -128.0, ALU.add))
-    for c in range(nch):
-        vec("S0_%d" % c, W[c], ["sqi"], ["S0_%d" % c], ts(land(0, c, "S"), T.sqi[:, C0[c]:C0[c] + W[c]], 128.0, ALU.add))
-        vec("E0_%d" % c, W[c], ["posi"], ["E0_%d" % c], ts(land(0, c, "E"), T.posi[:, C0[c]:C0[c] + W[c]], 0.0, ALU.is_equal))
+    vec("K0", LN, ["kni"], ["kin0"], ts(T.kin[:, 0:LN], T.kni[:], -128.0, ALU.add))
+    vec("L0", LN, ["posi"], ["L0_%d" % c for c in range(NCH)], lambda: V.tensor_copy(T.lst[:, 0:LN], T.posi[:]))
+    for c in range(NCH):
+        vec("S0_%d" % c, n, ["sqi"], ["S0_%d" % c], ts(land(0, c, "S"), T.sqi[:, c * n:c * n + n], 128.0, ALU.add))
+        vec("E0_%d" % c, n, ["posi", "cE"], ["E0_%d" % c], ts(land(0, c, "E"), T.posi[:, c * n:c * n + n], col(7), ALU.is_le))
+        for t in range(PLIES):
+            act("b%d_%d_0" % (t, c), n, ["one", "oh"], ["b%d_%d" % (t, c)], scaled(land(t, c, "b"), Mc("one", 0, n), oh(0)))
 
     def dst(k):
         rid, pid = topo.addr(T.cores[(rank + k) % N], core)
@@ -191,179 +223,168 @@ def build(g, T, core, topo):
         tr = RemoteDMATransfer(dst_ids=[dst(k) for k in range(1, PLIES)], dma_engine_mask=wide, remote_sem=T.sem.karr,
                                src=T.kin[:, 0:LN], dsts=[T.kin[:, k * LN:(k + 1) * LN] for k in range(1, PLIES)])
         return g.remote_dma_fused([tr], local_sem=T.sem.kgo)
-    ks = add("G", "ksend", ("r", 1), ["K0"], [], ksend, token=("kgo", ne))
-    add("X", "karr", ("x", 2), [], ["K%d" % k for k in range(1, PLIES)], None, token=("karr", ne * (PLIES - 1)), after=ks)
+    ks = add("G", "ksend", ("r", 1), ["kin0"], [], ksend, token=("kgo", ne))
+    add("X", "karr", ("x", 2), [], ["kin%d" % k for k in range(1, PLIES)], None, token=("karr", ne * (PLIES - 1)), after=ks)
 
-    for k in range(4):
-        a, b = T.tab[:, 4096 + 1024 * k:4096 + 1024 * (k + 1)], T.tab[:, 1024 * k:1024 * (k + 1)]
-        if k < PAR["negv"]:
-            vec("neg%d" % k, 512, ["tab"], ["neg%d" % k], ts(a, b, -1.0, ALU.mult))
-        else:
-            act("neg%d" % k, 1024, ["tab"], ["neg%d" % k], scaled(a, b, -1))
-
-    later = []
+    step = [0]
 
     def ply(t, c):
         last = t == PLIES - 1
-        q = "%d_%d" % (t, c)
-        n, c0 = W[c], C0[c]
+        q, p = "%d_%d" % (t, c), "%d_%d" % (t - 1, c)
+        c0 = c * n
         cs = slice(c0, c0 + n)
-        c240 = T.flo[:, 1:32 * n:32]
+        turn = (t * NCH + c) % 2
 
         def pl(buf, s):
             return buf[:, s * LN + c0:s * LN + c0 + n]
 
-        def r(k):
-            return slice(k * n, k * n + n)
+        def L(s):
+            return pl(T.lst, s)
+
+        def H(s):
+            return pl(T.hh, s)
         Sp, Ep, bp, Kp = land(t, c, "S"), land(t, c, "E"), land(t, c, "b"), pl(T.kin, t)
-        rS, rE, rK = "S" + q, "E" + q, "K%d" % t
-        w = 16 if t == 0 else 32
-        g0 = 32 * c0
+        rS, rE, rK = "S" + q, "E" + q, "kin%d" % t
 
-        def xend(s, i, j):
-            if s == 0:
-                return T.x0[:, 16 * (c0 + i) + 15:16 * (c0 + j):16]
-            return T.xs[:, g0 + 32 * i + 31:g0 + 32 * j:32]
+        def X(s, i=0, j=n):
+            return T.xs[:, 16 * (s * LN + c0 + i) + 15:16 * (s * LN + c0 + j):16]
 
-        def rx(s, i, j):
-            return cols("x%d_%d" % (min(s, 1), c), 32 * i, 32 * j)
-        R = [(M("I"), Kp, n), (M("I"), Sp, n), (M("nE"), Ep, n)]
-        rR = [rS, rE, rK, "I", "nE"]
+        def rx(s, i=0, j=n):
+            return cols("x%d_%d" % (s, c), 16 * i, 16 * j)
 
-        vec("kb" + q, n // 2, [rS, "thr"], ["kb" + q], ts(pl(T.kb, t), Sp, T.col[:, 1:2], ALU.is_ge, 2048.0, ALU.mult))
-        kb = (M("Bk"), pl(T.kb, t), n)
+        def wipe(out, nm, s):
+            return [(out, M(nm), H(s)), (out, M("n" + nm), H(s))]
+
+        def other(out, Z, kind):
+            terms = []
+            for s in range(1, t):
+                if s in PAR["keep"][kind]:
+                    terms = [(out, M("I"), kept(kind, s))] + wipe(out, "Diff", s) + [(out, M("I"), Z(s - 1))]
+                elif s == 1:
+                    terms = [(out, M("I"), Z(0))] + wipe(out, "Same", 1)
+                else:
+                    terms += [(out, M("nI"), Z(s - 1))] + wipe(out, "Diff", s) + [(out, M("I"), Z(s - 1))]
+            return terms + [(out, M("nI"), Z(t - 1))]
+
+        def kept(kind, s):
+            return pl(T.zs, s + PLIES * (kind == "a"))
         o0 = 2 * c0
-        A, B, O = bank("R", c), bank("Z", c), bank("off", c)
-        pa, pb, po = T[A], T[B], T[O]
+        ones = Mc("one", 0, n)
+        thr, raw, old, a0 = T.ps5[:, 0:n], T.ps0[:, 0:n], T.ps1[:, 0:n], T.ps2[:, 0:n]
+        rem, ins = T.ps4[:, 0:n], T.ps4[:, n:2 * n]
         if t == 0:
-            pe("R" + q, [(pa[:, r(0)], R)], rR, A)
-            pe("offp" + q, [(po[:, r(0)], R + [kb])], rR + ["Bk", "kb" + q], O)
-            vec("off" + q, n, [], ["off%d" % c], lambda: V.tensor_copy(T.off[:, o0:o0 + n], po[:, r(0)]), [O])
+            vec("H" + q, n // 2, [rS, "thr"], ["H" + q], ts(H(0), Sp, col(1), ALU.is_ge))
+            pe("offp" + q, [(old, M("I"), L(0)), (old, M("B"), H(0))], ["I", "B", "L" + q, "H" + q], "ps1", True)
+            vec("off" + q, n, [], ["off%d" % c], lambda: V.tensor_copy(T.off[:, o0 + n:o0 + 2 * n], old), ["ps1"])
         else:
-            p = "%d_%d" % (t - 1, c)
-            X = pl(T.lst, t - 1)
-            hl = [(M("nI"), pl(T.tl, s), n) for s in range(1, t)]
-            ha = [(M("nI"), pl(T.ta, s), n) for s in range(1, t)]
-            pe("Z" + q, [(pb[:, r(0)], hl + [(M("nI"), X, n)]),
-                         (pb[:, r(1)], ha + [(M("I"), c240, n), (M("nI"), xend(t - 1, 0, n), n)])],
-               ["I", "nI", "c240", "L" + p] + rx(t - 1, 0, n) + ["T%s%d_%d" % (k, s, c) for k in "la" for s in range(1, t)], B)
-            pe("R" + q, [(pb[:, r(2)], R)], rR, B)
-            vec("L" + q, n, [], ["L" + q], ts(pl(T.lst, t), pb[:, r(2)], 0.0, ALU.max), [B])
-            Lt = (M("I"), pl(T.lst, t), n)
-            pe("RX" + q, [(pb[:, r(3)], [(M("nI"), X, n), Lt])], ["I", "nI", "L" + p, "L" + q], B)
-            gs = [(pa[:, r(2)], [(M("nBk"), pl(T.kb, t - 1), n), kb])]
-            if last:
-                gs.append((pa[:, r(3)], [kb]))
-            pe("sig" + q, gs, ["Bk", "nBk", "kb" + q, "kb" + p], A)
-            if "sw" in PAR["scalar"]:
-                act("sw" + q, n, [], ["sw%d" % c], lambda pa=pa: S.activation(T.sw[:, cs], pa[:, r(2)], ACT.Abs, scale=1.0 / 2048), [A])
-            else:
-                vec("sw" + q, n, [], ["sw%d" % c], ts(T.sw[:, cs], pa[:, r(2)], 0.0, ALU.not_equal), [A])
-            vec("Tl" + q, n, ["sw%d" % c], ["Tl" + q], tt(pl(T.tl, t), pb[:, r(0)], T.sw[:, cs], ALU.mult), [B])
-            vec("eq" + q, n, ["Tl" + q], ["eq%d" % c], tt(T.eq[:, cs], pb[:, r(3)], pl(T.tl, t), ALU.is_equal), [B])
-            vec("Ta" + q, n, ["sw%d" % c], ["Ta" + q], tt(pl(T.ta, t), pb[:, r(1)], T.sw[:, cs], ALU.mult), [B])
-            eq = (M("nQ"), T.eq[:, cs], n)
-            pe2("offp" + q, [(po[:, 2 * n + 1:4 * n:2], [Lt, kb, eq]),
-                             (po[:, 2 * n:4 * n:2], [(M("I"), X, n), (M("Bk2"), pl(T.kb, t), n), (M("I"), pl(T.tl, t), n), eq])], 1,
-                ["I", "Bk", "Bk2", "kb" + q, "Tl" + q, "L" + p, "L" + q], ["nQ", "eq%d" % c], O)
-            vec("off" + q, 2 * n, [], ["off%d" % c], lambda: V.tensor_copy(T.off[:, o0:o0 + 2 * n], po[:, 2 * n:4 * n]), [O])
-        if t == 0:
-            vec("L" + q, n, [], ["L" + q], ts(pl(T.lst, t), pa[:, r(0)], 0.0, ALU.max), [A])
+            rh = ["I", "nI", "Same", "nSame", "Diff", "nDiff"] + ["H%d_%d" % (s, c) for s in range(t)]
+            rl = ["L%d_%d" % (s, c) for s in range(t)]
 
-        def closing(kind, X, rX, buf, nm, outbuf, dram):
-            hist = [(M("nI"), pl(buf, s), n) for s in range(1, PLIES)]
-            rh = [nm + "%d_%d" % (s, c) for s in range(1, PLIES)]
-            cz = [(M("I"), c240, n)] if kind == "a" else []
-            up = [(M("nI"), c240, n)] if kind == "a" else []
-            f = nm + "f%d" % c
-            B = bank("end" if kind == "c" or PAR["banks"] == "chunk" else "ZR"[c % 2], c)
-            pb = T[B]
-            pe("Zf" + kind + q, [(pb[:, r(0)], hist + cz + [(M("nI"), X, n)])], rh + rX + ["nI", "I", "c240"], B)
-            vec(f, n, ["bb%d" % c], [f], tt(pl(buf, PLIES), pb[:, r(0)], T.bb[:, cs], ALU.mult), [B])
-            pe("Cf" + kind + q, [(pb[:, r(1)], up + [(M("I"), X, n), (M("I"), pl(buf, PLIES), n)]),
-                                 (pb[:, r(2)], hist + [(M("nI"), pl(buf, PLIES), n)])], rh + rX + [f, "nI", "I", "c240"], B)
+            def ahead(kind, out, Z, reads, bank):
+                keep = t in PAR["keep"][kind]
+                pe("pre" + kind + q, other(out, Z, kind), rh + reads + ["Z%s%d_%d" % (kind, s, c) for s in range(t)], bank, True, keep)
+                if keep:
+                    z = "Z" + kind + q
+                    vec(z, n, [], [z], lambda: V.tensor_copy(kept(kind, t), out), [bank])
+                    pe("re" + kind + q, [(out, M("I"), kept(kind, t))], [z], bank, True, False)
+            pe("thr" + q, [(thr, M("Th"), H(t - 1))], ["Th1", "Th2", "H" + p], "ps5", True)
+            vec("H" + q, n, [rS], ["H" + q], tt(H(t), Sp, thr, ALU.is_ge), ["ps5"])
+            pe("Re" + q, [(raw, M("I"), Kp)], [rK, "I"], "ps0", True, False)
+            pe("R" + q, [(raw, M("I"), Sp), (raw, M("nE"), Ep)], [rS, rE, "nE"], "ps0")
+            vec("L" + q, n, [], ["L" + q], ts(L(t), raw, 0.0, ALU.max), ["ps0"])
+            ahead("c", old, L, rl, "ps1")
+            pe("Op" + q, wipe(old, "Same", t) + [(old, M("I"), L(t - 1))], ["H" + q], "ps1")
+            eq = T.eq[:, cs]
+            vec("eq" + q, n, ["L" + q], ["eq%d" % c], tt(eq, L(t), old, ALU.is_equal), ["ps1"])
+            pe("prer" + q, [(rem, M("I"), kept("c", t))] if t in PAR["keep"]["c"] else other(rem, L, "c"),
+               rh + rl + ["Zc%d_%d" % (s, c) for s in range(t + 1)], "ps4", True, False)
+            pe("offe" + q, wipe(rem, "Same", t) + [(rem, M("I"), L(t - 1)), (rem, M("B"), H(t)), (ins, M("B"), H(t))],
+               ["B", "H" + q], "ps4", False, False)
+            pe("offp" + q, [(ins, M("I"), L(t)), (rem, M("nQ"), eq), (ins, M("nQ"), eq)], ["nQ", "eq%d" % c, "L" + q], "ps4")
+            vec("off" + q, 2 * n, [], ["off%d" % c], lambda: V.tensor_copy(T.off[:, o0:o0 + 2 * n], T.ps4[:, 0:2 * n]), ["ps4"])
+            ahead("a", a0, X, sum([rx(s) for s in range(t)], []), "ps2")
+            pe("posa" + q, wipe(a0, "Same", t) + [(a0, M("I"), X(t - 1))], ["H" + q], "ps2", False, False)
+
+        def closing(kind, Z, reads, outbuf, dram):
+            early, late = [], []
             for b in range(2):
-                act("o%s%d_%d" % (kind, b, c), n, [], ["o%s%d_%d" % (kind, b, c)],
-                    scaled(outbuf[:, o0 + b:o0 + 2 * n:2], pb[:, r(1 + b)], 1), [B])
-            add("S", "st" + kind + q, ("d", 2.0), ["o%s%d_%d" % (kind, b, c) for b in range(2)], [],
-                lambda: g.sync.dma_start(dram[:, o0:o0 + 2 * n], outbuf[:, o0:o0 + 2 * n]), token=("outs", 16 * 3 * nch))
+                out = T.ps7[:, b:2 * n:2]
+                early += [(out, M("I"), kept(kind, t))] + wipe(out, "K%d" % b, t - 1) + [(out, M("I"), Z(t - 1))]
+                late += [(out, M("nI"), Z(t))] + wipe(out, "K%d" % b, t) + [(out, M("I"), Z(t))]
+            pe("Ce" + kind + q, early, ["Z" + kind + q, "K0", "nK0", "K1", "nK1"], "ps7", True, False)
+            pe("Cl" + kind + q, late, reads + ["H" + q], "ps7")
+            act("o" + kind + q, 2 * n, [], ["o" + kind + q], scaled(outbuf[:, o0:o0 + 2 * n], T.ps7[:, 0:2 * n], 1.0), ["ps7"])
+            add("S", "st" + kind + q, ("d", 2.0), ["o" + kind + q], [],
+                lambda: g.sync.dma_start(dram[:, o0:o0 + 2 * n], outbuf[:, o0:o0 + 2 * n]), token=("outs", 16 * 3 * NCH))
 
         if last:
-            vec("bb" + q, n, [], ["bb%d" % c], ts(T.bb[:, cs], pa[:, r(3)], 0.0, ALU.not_equal), [A])
-            closing("c", pl(T.lst, t), ["L" + q], T.tl, "Tl", T.oc, T.yc)
+            closing("c", L, ["L" + q], T.oc, T.yc)
 
-        win = T.tab[:, 0:4096] if t == 0 else T.tab[:, 0:8192]
-        rt = ["tab"] + ([] if t == 0 else ["neg%d" % k for k in range(4)])
-        d = (t * nch + c) % ND1
-        f0 = 32 * CW * d
-        i = 0
-        D1 = bank("d1", c)
-        pd = T[D1]
-        for h, part in enumerate(pieces(n, *PAR["gat0" if t == 0 else "gat1"])):
-            i0 = i
-            for e, k in part:
-                j = i + k
-                src = T.off[:, o0 + i * w // 16:o0 + j * w // 16]
-                out = T.gw[:, g0 + i * w:g0 + j * w]
-                if e == "A":
-                    fn = lambda out=out, src=src: S.activation(out, win.indirect(src), ACT.Copy)
+        for half in range(int(t == 0), 2):
+            d = step[0] % ND1
+            step[0] += 1
+            f0, g0, s = 16 * n * d, 16 * (2 * c0 + half * n), t if half else PLIES
+            i = 0
+            for h, part in enumerate(pieces(n, *PAR.get("gat%s_%d" % (q, half), PAR["gat0" if t == 0 else "gat%d" % (1 + half)]))):
+                i0 = i
+                for e, k in part:
+                    j = i + k
+                    src = T.tab[:].indirect(T.off[:, o0 + half * n + i:o0 + half * n + j])
+                    out = T.gw[:, g0 + 16 * i:g0 + 16 * j]
+                    sign = 2.0 * half - 1.0
+                    add(e, "gat%s_%d_%d" % (q, half, i), ("gat", 16 * k), ["tab0", "tab1", "none0", "none1", "off%d" % c], cols("gw%d_%d" % (c, half), 16 * i, 16 * j),
+                        scaled(out, src, sign) if e == "A" else ts(out, src, sign, ALU.mult))
+                    i = j
+                m, qh = i - i0, "%s_%d_%d" % (q, half, h)
+                rg, rf = cols("gw%d_%d" % (c, half), 16 * i0, 16 * i), cols("flo%d" % d, 16 * i0, 16 * i)
+                first = T.gw[:, g0 + 16 * i0:g0 + 16 * i:16]
+                ffirst = T.flo[:, f0 + 16 * i0:f0 + 16 * i:16]
+                if t == 0:
+                    vec("d1" + qh, m // 2, rg, rf, ts(ffirst, first, 0.0, ALU.max))
                 else:
-                    fn = lambda out=out, src=src: V.tensor_copy(out, win.indirect(src))
-                add(e, "gat%s_%d" % (q, i), ("gat", k * w), rt + ["off%d" % c], cols("gw%d" % c, i * w, j * w), fn)
-                i = j
-            m, qh = i - i0, "%s_%d" % (q, h)
-            rg, rf = cols("gw%d" % c, i0 * w, i * w), cols("flo%d" % d, i0 * 32, i * 32)
-            first = T.gw[:, g0 + i0 * w:g0 + i * w:w]
-            ffirst = T.flo[:, f0 + 32 * i0:f0 + 32 * i:32]
-            if t == 0:
-                vec("d1" + qh, m // 2, rg, rf, ts(ffirst, first, -240.0, ALU.add, -240.0, ALU.max))
-                floor = T.flo[:, f0 + 32 * i0:f0 + 32 * i:2]
-            else:
-                ta = T.ta[:, t * LN + c0 + i0:t * LN + c0 + i]
-                pe2("d1p" + qh, [(pd[:, i0:i], [(M("I"), xend(t - 1, i0, i), 64), (M("I"), ta, 64), (M("I"), first, 64)])], 1,
-                    ["I", "Ta" + q] + rx(t - 1, i0, i), rg, D1)
-                vec("d1" + qh, m, [], rf, ts(ffirst, pd[:, i0:i], -240.0, ALU.max), [D1])
-                floor = T.flo[:, f0 + 32 * i0:f0 + 32 * i]
-            if PAR["reset"] == "G":
-                gps("rst" + qh, m, [], rg, lambda first=first, m=m: g.iota(first, [[0, m]], -1024, 0, allow_small_or_imprecise_dtypes=True))
-            else:
-                vec("rst" + qh, m // 2, [], rg, lambda first=first: V.memset(first, -1024.0))
-            xo = T.x0[:, 16 * (c0 + i0):16 * (c0 + i)] if t == 0 else T.xs[:, g0 + 32 * i0:g0 + 32 * i]
-            vec("scan" + qh, w * m // 2, rg + rf, rx(t, i0, i),
-                lambda xo=xo, a=T.gw[:, g0 + i0 * w:g0 + i * w], floor=floor: V.tensor_tensor_scan(xo, a, floor, -240.0, ALU.add, ALU.max))
-        xnow, rxn = xend(t, 0, n), rx(t, 0, n)
+                    B = "ps7" if half and not last else "ps2"
+                    to = T[B][:, i0:i]
+                    pe("d1p" + qh, [(to, M("I"), X(PLIES, i0, i))] * half + [(to, M("I"), first)], rg + rx(PLIES, i0, i) * half, B, half == 1)
+                    vec("d1" + qh, m, [], rf, ts(ffirst, to, 0.0, ALU.max), [B])
+                if PAR["reset"][half] == "G":
+                    gps("rst" + qh, m, [], rg, lambda first=first, m=m: g.iota(first, [[0, m]], -1024, 0, allow_small_or_imprecise_dtypes=True))
+                else:
+                    vec("rst" + qh, m // 2, [], rg, fill(first, -1024.0))
+                for a in range(i0, i, PAR["run"][half]):
+                    b = min(i, a + PAR["run"][half])
+                    vec("scan" + qh, 8 * (b - a), cols("gw%d_%d" % (c, half), 16 * a, 16 * b) + cols("flo%d" % d, 16 * a, 16 * b), rx(s, a, b),
+                        lambda xo=T.xs[:, 16 * (s * LN + c0 + a):16 * (s * LN + c0 + b)], w=T.gw[:, g0 + 16 * a:g0 + 16 * b],
+                        floor=T.flo[:, f0 + 16 * a:f0 + 16 * b]: V.tensor_tensor_scan(xo, w, floor, 0.0, ALU.add, ALU.max))
         y = T.yv[:, cs]
-        vec("y" + q, n // 2, rxn, ["y%d" % c], ts(y, xnow, 240.0, ALU.add, 127.0, ALU.min))
-        Sc, G, A = bank("sc", c), bank("G", c), bank("raw", c)
-        sc, pg, pa = T[Sc], T[G], T[A]
-        pe2("scp" + q, [(sc[0:n, 0:128], [(Ep, M("nM"), 128), (y, M("U1"), 128)])], 1, [rE, "nM"], ["y%d" % c, "U1"], Sc)
-        pe("vlp" + q, [(sc[64:64 + n, 0:128], [(y, M("V1"), 128)])], ["y%d" % c, "V1", "shut" + Sc], Sc)
-        pm = T.pm[:, 128 * c:128 * c + 128]
-        vec("max" + q, 128, ["tie"], ["pm%d" % c],
-            lambda: V.tensor_tensor_scan(pm, T.tie[:], sc[:, 0:128], 0.0, ALU.add, ALU.max), [Sc])
-        pw = T.pw[:, 8 * c:8 * c + 8]
-        vec("maw" + q, 8, ["pm%d" % c], ["pw%d" % c], lambda: V.tensor_copy(pw, T.pm[:, 128 * c + 15:128 * c + 128:16]))
-        m0, rm = 144 * ((t * nch + c) % 2) + 16, "top%d" % ((t * nch + c) % 2)
-        add("V", "top" + q, ("gat", 128), ["pm%d" % c, "pw%d" % c, "pe16"], [rm],
-            lambda: V.tensor_tensor(T.top[:, m0:m0 + 128], pw.indirect(T.pu[:, 8:16]), pm, ALU.is_equal))
-        k1 = 128 * MATS.index("one")
-        pe("Gre" + q, [(pg[:, 0:128], [(T.nk[:], T.mat[:, k1:k1 + 128], 128)])], ["nk", "one"], G, True, False)
-        pe("Gr" + q, [(pg[:, 0:128], [(T.top[:, m0 - 1:m0 + 127], M("I2"), 128), (T.top[:, m0:m0 + 128], M("nI2"), 128)])],
-           [rm, "I2", "nI2"], G, False, True)
-        vec("b" + q, n, [rS], ["b" + q], tt(bp, pg[:, r(0)], Sp, ALU.min), [G])
+        vec("y" + q, n // 2, rx(t), ["y%d" % c], ts(y, X(t), 127.0, ALU.min))
+        if last:
+            closing("a", X, rx(t), T.oa, T.ya)
+        Sc, G, A = "ps3", "ps6", "ps6"
+        sc, pg, pa, pz = T[Sc], T[G], T[A][:, 128:128 + n], T[A][:, 192:192 + n]
+        ro, di = (0, n) if t % 2 == 0 else (n, 0)
+        eb = (t * LN + c0) * 3 + n - ro
+        pe("sce" + q, [(sc[:, 0:DW], T.land[:, eb:eb + 2 * n], D(3))], ["C", rE, "b" + q], Sc, True, False, DW)
+        pe("scp" + q, [(sc[ro:ro + n, 0:DW], y, D(1)), (sc[di:di + n, 0:DW], y, D(2))], ["y%d" % c, "Ud", "Vd"], Sc, False, 2, DW)
+        r0 = 128 * turn
+        z = T.zz[:, r0:r0 + 128]
+        vec("lap1" + q, 128, ["zer"], ["ra%d" % turn],
+            lambda: V.tensor_tensor_scan(T.ra[:, r0:r0 + 128], sc[:, 0:128], D(4, 0, 128), 0.0, ALU.add, ALU.max), [Sc])
+        vec("round" + q, 8, ["ra%d" % turn], ["rb%d" % turn],
+            tt(T.rb[:, r0:r0 + 128:16], T.ra[:, r0 + 15:r0 + 128:16], sc[:, 128:DW], ALU.add), [Sc])
+        vec("lap2" + q, 128, ["rb%d" % turn], ["z%d" % turn],
+            lambda: V.tensor_tensor_scan(z, sc[:, 0:128], T.rb[:, r0:r0 + 128], 0.0, ALU.add, ALU.max), [Sc])
+        pe("Gr" + q, [(pg[:, 0:128], z, M("I2"))], ["z%d" % turn, "I2"], G, True, True, 128)
+        vec("b" + q, n, [rS], ["b" + q], tt(bp, pg[:, ro:ro + n], Sp, ALU.min), [G])
         sth = T.sth[:, cs]
-        vec("sth" + q, n, ["stf", "win"], ["sth%d" % c], ts(sth, pg[:, 64:64 + n], T.col[:, 3:4], ALU.is_equal, T.col[:, 2:3], ALU.mult), [G])
-        js = (M("J"), sth, n)
-        pe2("raw" + q, [(pa[:, r(0)], [(M("J"), Sp, n), (M("nJ"), bp, n), js]),
-                        (pa[:, r(1)], [(M("J"), Sp, n), (M("nJ1"), bp, n), js])], 2,
-            ["J", rS], ["nJ", "nJ1", "b" + q, "sth%d" % c], A)
-        wn = T.wn[:, cs]
-        vec("wn" + q, n, [], ["wn%d" % c], ts(wn, pa[:, r(0)], 256.0, ALU.is_ge, 128.0, ALU.mult), [A])
+        vec("sth" + q, n, ["stf", "win"], ["sth%d" % c], ts(sth, pg[:, di:di + n], col(3), ALU.is_equal, col(2), ALU.mult), [G])
+        pe("raw" + q, [(pa, M("nJ"), Sp), (pa, M("J"), bp), (pa, M("nJ"), sth), (pa, M("MG"), ones), (pa, M("nMG"), ones),
+                       (pa, M("J"), Sp), (pa, M("nJ1"), bp), (pa, M("J"), sth)],
+           ["J", "nJ", "nJ1", "MG", "nMG", "b" + q, "sth%d" % c], A, True)
         ob = 3 * c0
         hit = T.outb[:, ob + n:ob + 2 * n]
         mov = T.outb[:, ob + 2 * n:ob + 3 * n] if t % 2 == 0 else T.outb[:, ob:ob + n]
-        vec("mov" + q, n, ["wn%d" % c], ["mov%d" % c], tt(mov, pa[:, r(1)], wn, ALU.subtract), [A])
-        vec("hit" + q, n, ["wn%d" % c], ["hit%d" % c], tt(hit, pa[:, r(1)], wn, ALU.is_equal), [A])
+        vec("hit" + q, n, [], ["hit%d" % c], ts(hit, pa, -191.5, ALU.is_equal), [A])
+        vec("mov" + q, n, [], ["mov%d" % c], ts(mov, pa, 191.5, ALU.add), [A])
         if not last:
             u = "%d_%d" % (t + 1, c)
             lo, lo1, h = (t * LN + c0) * 3, ((t + 1) * LN + c0) * 3, n if t % 2 == 0 else 0
@@ -376,21 +397,17 @@ def build(g, T, core, topo):
             s = add("G", "snd" + q, ("r", 1), ["mov%d" % c, "hit%d" % c, "b" + q, rE], [], onward, token=("go%d" % c, ne * (t + 1)))
             add("X", "arr" + u, ("x", 1), [], ["S" + u, "E" + u], None, token=("arr" + u, ne), after=s)
         else:
-            later.append(((t, c, nch), lambda: closing("a", xnow, rxn, T.ta, "Ta", T.oa, T.ya)))
-            vec("snew" + q, 2 * n, ["mov%d" % c, "b" + q], ["snew%d" % c], tt(T.snew[:, cs], mov, bp, ALU.max))
-            pe("ylp" + q, [(pa[:, r(0)], [(M("I"), Kp, n), (M("nE"), Ep, n), (M("nE"), hit, n), (M("I"), T.snew[:, cs], n)])],
-               [rK, rE, "I", "nE", "hit%d" % c, "snew%d" % c], A)
-            act("yl" + q, n, [], ["ol%d" % c], lambda: S.activation(T.ol[:, cs], pa[:, r(0)], ACT.Relu), [A])
+            pe("ylp" + q, [(pz, M("I"), mov), (pz, M("IB"), bp), (pz, M("nIB"), bp), (pz, M("I"), bp), (pz, M("I"), Kp),
+                           (pz, M("nE"), Ep), (pz, M("nE"), hit)], ["IB", "nIB", rK, rE, "mov%d" % c, "hit%d" % c], A, True)
+            act("yl" + q, n, [], ["ol%d" % c], lambda: S.activation(T.ol[:, cs], pz, ACT.Relu), [A])
             add("S", "stl" + q, ("d", 2.0), ["ol%d" % c], [], lambda: g.sync.dma_start(T.yl[:, cs], T.ol[:, cs]),
-                token=("outs", 16 * 3 * nch))
+                token=("outs", 16 * 3 * NCH))
 
+    now.append(True)
     for t in range(PLIES):
-        for c in range(nch):
-            now[0] = (t, c, nch)
+        for c in range(NCH):
+            now[0] = (t, c)
             ply(t, c)
-    for at, fn in later:
-        now[0] = at
-        fn()
     return ops
 
 
@@ -440,7 +457,7 @@ def times(o, par):
         a = 0.16 + 2 * x * par["cyc"]
         return a, a
     if k == "p":
-        a = sum(x) * par["pe"] + len(x) * par["pemm"]
+        a = x * par["pe"]
         return a, a + par["pefix"]
     if k == "d":
         return 0.1, x
@@ -458,16 +475,13 @@ def schedule(ops, deps, par):
             nxt[j].append(i)
     way = [0.0] * m
     for i in range(m - 1, -1, -1):
-        t, c, nch = ops[i]["chunk"]
-        due = -(c * par["beat0"] if t == 0 else nch * par["beat0"] + ((t - 1) * nch + c) * par["beat"])
+        t, c = ops[i]["chunk"]
+        due = -(c * par["beat0"] if t == 0 else NCH * par["beat0"] + ((t - 1) * NCH + c) * par["beat"])
         way[i] = max([way[j] + par["hop"] for j in nxt[i]] or [due]) + tm[i][1]
         if ops[i]["name"].startswith("snd"):
             way[i] = due + tm[i][1]
         if ops[i]["name"] == "ksend":
             way[i] = par["kway"]
-    rng = np.random.default_rng(par["seed"])
-    for i in range(m):
-        way[i] += float(rng.random()) * par["noise"] + par.get("bias", {}).get(i, 0.0)
     done, left = [None] * m, [len(d) for d in deps]
     ready = [0.0] * m
     free = {e: 0.0 for e in "VAPGS"}
@@ -494,7 +508,123 @@ def schedule(ops, deps, par):
         if i in arrive:
             order.append(arrive[i])
             finish(arrive[i], now, now + tm[arrive[i]][1])
-    return order, max(done)
+    return justify(ops, deps, par, order)
+
+
+def justify(ops, deps, par, order):
+    m = len(ops)
+    tm = [times(o, par) for o in ops]
+    pre = [[(j, tm[j][1] + par["hop"] if waits(ops, i, j) else tm[j][0]) for j in deps[i]] for i in range(m)]
+    for i, o in enumerate(ops):
+        if o["after"] is not None:
+            pre[i] = [(o["after"], 0.0)]
+    suc = [[] for _ in ops]
+    for i in range(m):
+        for j, lag in pre[i]:
+            suc[j].append((i, lag))
+
+    def pack(seq, back):
+        at, busy = [0.0] * m, {}
+        for i in seq:
+            hold = tm[i][0]
+            s = max([at[j] + lag for j, lag in suc[i]] + [tm[i][1]]) - hold if back else max([at[j] + lag for j, lag in pre[i]] + [0.0])
+            if hold:
+                line = busy.setdefault(ops[i]["eng"], [])
+                k = 0
+                for k, (a, b) in enumerate(line + [(1e9, 1e9)]):
+                    if s + hold <= a + 1e-9:
+                        break
+                    s = max(s, b)
+                line.insert(k, (s, s + hold))
+            at[i] = s + hold if back else s
+        return at
+    best = None
+    for _ in range(par["passes"]):
+        at = pack(order, False)
+        rank = {i: k for k, i in enumerate(order)}
+        order = sorted(order, key=lambda i: (at[i], rank[i]))
+        end = max(at[i] + tm[i][1] for i in range(m))
+        if best is None or end < best[1]:
+            best = (order, end, [at[i] + tm[i][1] for i in range(m)])
+        rank = {i: k for k, i in enumerate(order)}
+        late = pack(sorted(order, key=lambda i: (-at[i], -rank[i])), True)
+        order = sorted(order, key=lambda i: (-late[i], rank[i]))
+    return best
+
+
+def polish(ops, deps, par, order):
+    m = len(ops)
+    rng = np.random.default_rng(par["seed"])
+    eng = ["VAPGSX".index(o["eng"]) for o in ops]
+    pre, hold, res = [], [], []
+    for _, guess in COSTS:
+        cost = dict(par, **guess)
+        tm = [times(o, cost) for o in ops]
+        pre.append([[(o["after"], 0.0)] if o["after"] is not None else
+                    [(j, tm[j][1] + cost["hop"] if waits(ops, i, j) else 0.0) for j in deps[i]] for i, o in enumerate(ops)])
+        hold.append([x[0] for x in tm])
+        res.append([x[1] for x in tm])
+    before = [set(j for j, _ in pre[0][i]) for i in range(m)]
+    after = [set() for _ in ops]
+    for i in range(m):
+        for j in before[i]:
+            after[j].add(i)
+    ends = [i for i in range(m) if not after[i]]
+
+    def run(seq, k, r, old):
+        at, by = (list(old[1]), list(old[2])) if old else ([0.0] * m, [-1] * m)
+        free, last = [0.0] * 6, [-1] * 6
+        for i in seq[:r]:
+            free[eng[i]], last[eng[i]] = at[i] + hold[k][i], i
+        for i in seq[r:]:
+            e = eng[i]
+            s, w = (0.0, -1) if e == 5 else (free[e], -2 - last[e])
+            for j, lag in pre[k][i]:
+                if at[j] + lag > s:
+                    s, w = at[j] + lag, j
+            at[i], by[i] = s, w
+            free[e], last[e] = s + hold[k][i], i
+        return max((at[i] + res[k][i], i) for i in ends), at, by
+
+    def pairs(x):
+        out, i = [], x[0][1]
+        while i >= 0:
+            w = x[2][i]
+            if w <= -2:
+                out.append((-2 - w, i))
+            i = -2 - w if w <= -2 else w
+        return out
+
+    def score(seq, r, old):
+        rs = [run(seq, k, r, old and old[k]) for k in range(len(COSTS))]
+        return sum(c[0] * x[0][0] for c, x in zip(COSTS, rs)), rs
+    cur, rs = score(order, 0, None)
+    best, crit = (cur, order), [pairs(x) for x in rs]
+    for u in rng.random((par["tries"], 5)).tolist():
+        a = crit[int(u[0] * len(COSTS))]
+        if not a:
+            continue
+        j, i = a[int(u[1] * len(a))]
+        r, p = order.index(j), order.index(i)
+        far, up = max(0, int(u[2] * 3)), u[3] < 0.5
+        while far and (r > 0 if up else p < m - 1):
+            r, p = (r - 1, p) if up else (r, p + 1)
+            far -= eng[order[r if up else p]] == eng[i]
+        mid = order[r:p + 1]
+        along = {i if up else j}
+        for x in (reversed(mid) if up else mid):
+            if (after if up else before)[x] & along:
+                along.add(x)
+        if (j if up else i) in along:
+            continue
+        new = order[:r] + [x for x in mid if (x in along) == up] + [x for x in mid if (x in along) != up] + order[p + 1:]
+        c, nr = score(new, r, rs)
+        if c <= cur or u[4] < math.exp((cur - c) / par["warm"]):
+            order, cur, rs = new, c, nr
+            crit = [pairs(x) for x in rs]
+            if c < best[0]:
+                best = (c, order)
+    return best[1]
 
 
 PLAN = {}
@@ -506,7 +636,7 @@ def rank_program(g, core, T, topo):
     ops = build(g, T, core, topo)
     if not PLAN:
         PLAN["deps"] = depend(ops)
-        PLAN["order"] = schedule(ops, PLAN["deps"], PAR)[0]
+        PLAN["order"] = polish(ops, PLAN["deps"], PAR, schedule(ops, PLAN["deps"], PAR)[0])
     deps = PLAN["deps"]
     queue = {"V": g.vector, "A": g.scalar, "P": g.tensor, "G": g, "S": g.sync}
     known = {e: {} for e in queue}

import math
import numpy as np
from concourse.bass import DstId, RemoteDMATransfer
from concourse.mybir import AluOpType, AxisListType, ActivationFunctionType

ALU = AluOpType
ACT = ActivationFunctionType
N, LN, PLIES = 8, 256, 5
NCH, CW = 4, 64
ND1 = 2
BIG = 2.0 ** 40
MAGIC = 1.5 * 2.0 ** 30
PEN = 2.0 ** 23
DW = 136
PAR = {
    "gat0": (0, 0, 64), "gat1": (16, 0, 64), "gat2": (0, 0, 64),
    "gat0_0_1": (32, 0, 64), "gat1_0_0": (32, 0, 64), "gat4_3_1": (16, 0, 64),
    "run": (32, 32),
    "reset": "VV",
    "keep": {"c": (2, 3, 4), "a": (3, 4)},
    "hop": 0.15, "fix": 0.0, "cyc": 0.00104, "gat": 1.56, "pe": 0.0005, "pefix": 0.12, "issue": 0.8, "wire": 2.0,
    "beat0": 2.2, "beat": 3.2, "kway": 3.0, "look": 0.0, "passes": 3, "tries": 22000, "warm": 0.04, "seed": 0,
}
COSTS = [(2.0, {"pe": 0.00048}),
         (1.0, {"cyc": 0.00095, "gat": 1.3, "pe": 0.0008, "hop": 0.13, "wire": 2.1}),
         (0.7, {"cyc": 0.0009, "gat": 1.5, "pe": 0.00045, "hop": 0.1, "issue": 1.0, "wire": 3.0})]
MATS = ["one", "I", "nI", "J", "nJ", "nJ1", "Bk", "B", "IK", "nE", "nQ", "I2", "IP", "U1", "V1", "UT", "VT", "Th",
        "JB", "nJB", "Same", "nSame", "Diff", "nDiff", "K0", "nK0", "K1", "nK1", "MG", "nMG", "IB", "nIB"]

SCRATCH = {
    "tab": ("sbuf", [128, 4096], "bfloat16"),
    "posi": ("sbuf", [128, LN], "int32"), "sqi": ("sbuf", [128, LN], "int32"), "kni": ("sbuf", [128, LN], "int32"),
    "uv": ("sbuf", [128, 32], "bfloat16"), "sti": ("sbuf", [128, 8], "int32"), "col": ("sbuf", [128, 16], "float32"),
    "pi": ("sbuf", [128, 16], "int32"), "pu": ("sbuf", [128, 8], "uint16"), "oh": ("sbuf", [128, 32], "float32"),
    "mat": ("sbuf", [128, 128 * len(MATS)], "bfloat16"),
    "dm": ("sbuf", [128, 5 * 272], "bfloat16"), "rb": ("sbuf", [128, 256], "float32"), "ra": ("sbuf", [128, 256], "float32"), "zz": ("sbuf", [128, 256], "bfloat16"),
    "kin": ("sbuf", [128, PLIES * LN], "bfloat16"),
    "land": ("sbuf", [128, PLIES * 3 * LN], "bfloat16"), "outb": ("sbuf", [128, 3 * LN], "bfloat16"),
    "hh": ("sbuf", [128, PLIES * LN], "bfloat16"), "eq": ("sbuf", [128, LN], "bfloat16"), "yv": ("sbuf", [128, LN], "bfloat16"),
    "sth": ("sbuf", [128, LN], "float16"), "lst": ("sbuf", [128, PLIES * LN], "float16"), "zs": ("sbuf", [128, 2 * PLIES * LN], "float16"),
    "off": ("sbuf", [128, 2 * LN], "uint16"),
    "gw": ("sbuf", [128, 32 * LN], "bfloat16"), "xs": ("sbuf", [128, (PLIES + 1) * 16 * LN], "float16"),
    "flo": ("sbuf", [128, ND1 * 16 * CW], "float16"),
    "ol": ("sbuf", [128, LN], "float32"), "oa": ("sbuf", [128, 2 * LN], "float32"), "oc": ("sbuf", [128, 2 * LN], "float32"),
}
for _c in range(8):
    SCRATCH["ps%d" % _c] = ("psum", [128, 512], "float32")
SEMAPHORES = (["cV", "cA", "cP", "cG", "ldp", "ldw", "ldf", "flo", "outs", "karr", "kgo"] + ["go%d" % c for c in range(NCH)]
              + ["arr%d_%d" % (t, c) for t in range(1, PLIES) for c in range(NCH)])


def pieces(n, v, tail, most):
    parts = []
    for m, k in ([(n - tail, 0), (tail, v)] if tail else [(n, v)]):
        a = m - k
        cnt = -(-a // most)
        cut = [4 * (a * j // cnt // 4) for j in range(cnt)] + [a]
        parts.append(([("V", k)] if k else []) + [("A", cut[j + 1] - cut[j]) for j in range(cnt)])
    return parts


def build(g, T, core, topo):
    rank = T.rank_of(core)
    ops = []
    now = [(0, 0)]
    n = CW
    V, S, P = g.vector, g.scalar, g.tensor

    def add(eng, name, cost, reads, writes, fn, banks=(), token=None, after=None):
        ops.append({"eng": eng, "name": name, "cost": cost, "r": list(reads), "w": list(writes), "fn": fn,
                    "banks": list(banks), "token": token, "after": after, "chunk": now[0], "ply": len(now) > 1,
                    "kind": name.replace("%d_%d" % now[0], ":").replace(":_", "").split("_")[0].replace(":", "")})
        return len(ops) - 1

    def M(name):
        k = MATS.index(name)
        return T.mat[:, 128 * k:128 * k + 128]

    def Mc(name, a, b, s=1):
        k = 128 * MATS.index(name)
        return T.mat[:, k + a:k + b:s]

    def D(k, a=0, b=DW, s=1):
        return T.dm[:, 272 * k + a:272 * k + b:s]

    def vec(name, cyc, reads, writes, fn, banks=()):
        add("V", name, ("v", max(64, cyc)), reads, writes, fn, banks)

    def act(name, cyc, reads, writes, fn, banks=()):
        add("A", name, ("v", max(64, cyc)), reads, writes, fn, banks)

    def gps(name, cyc, reads, writes, fn):
        add("G", name, ("g", cyc), reads, writes, fn)

    def pe(name, terms, reads, bank, begin=False, end=True, cyc=n):
        def fn():
            last = None
            for k, (out, a, b) in enumerate(terms):
                last = P.matmul(out, a, b, begin and k == 0, end and k >= len(terms) - end)
            return last
        add("P", name, ("p", cyc * len(terms)), reads + ["acc" + bank], ["acc" + bank], fn, [bank])

    def ts(out, in0, s1, op0, s2=None, op1=None):
        if op1 is None:
            return lambda: V.tensor_scalar(out, in0, s1, None, op0)
        return lambda: V.tensor_scalar(out, in0, s1, s2, op0, op1)

    def tt(out, a, b, op):
        return lambda: V.tensor_tensor(out, a, b, op)

    def scaled(out, in_, k):
        return lambda: S.activation(out, in_, ACT.Copy, scale=k)

    def fill(out, k):
        return lambda: V.memset(out, k)

    def put(out, pattern, value, base):
        return lambda: g.affine_select(out, out, pattern, ALU.not_equal, value, base, 1)

    def cols(name, a, b):
        return ["%s:%d" % (name, k) for k in range(a // 64, (b + 63) // 64)]

    def col(k):
        return T.col[:, k:k + 1]

    def oh(k):
        return T.oh[:, 16 + k:17 + k]

    for b in range(2):
        add("S", "ldf%d" % b, ("d", 4.8 - 0.1 * b), [], ["tab%d" % b],
            lambda o=2048 * b: g.sync.dma_start(T.tab[:, o + 128:o + 2048], T.feat[:, o + 128:o + 2048]), token=("ldf", 32))
        vec("tab%d" % b, 64, [], ["none%d" % b], fill(T.tab[:, 2048 * b:2048 * b + 128], 0.0))
    add("A", "ldp", ("d", 2.0), [], ["posi"], lambda: S.dma_start(T.posi[:], T.pos[:]), token=("ldp", 16))
    add("S", "ldu", ("d", 2.0), [], ["u"], lambda: g.sync.dma_start(T.uv[:, 0:16], T.u[:]), token=("ldw", 48))
    add("S", "ldv", ("d", 2.0), [], ["v"], lambda: g.sync.dma_start(T.uv[:, 16:32], T.v[:]), token=("ldw", 48))
    add("S", "lds", ("d", 2.0), [], ["sti"], lambda: g.sync.dma_start(T.sti[:, 0:1], T.step[:]), token=("ldw", 48))

    blk = [[-16, 8], [0, 16]]
    dia = [[-1, 128]]
    vec("one", 64, [], ["one"], fill(M("one"), 1.0))
    gps("I", 128, ["one"], ["I"], lambda: g.affine_select(M("I"), M("one"), dia, ALU.is_equal, 0.0, 0, 1))
    gps("Bk", 128, ["one"], ["Bk"], lambda: g.affine_select(M("Bk"), M("one"), blk, ALU.is_equal, 0.0, 0, 1))
    gps("J0", 128, ["one"], ["J"], lambda: g.affine_select(M("J"), M("one"), blk, ALU.is_ge, 0.0, 0, 1))
    gps("J1", 128, ["J"], ["J"], lambda: g.affine_select(M("J"), M("J"), [[16, 8], [0, 16]], ALU.is_ge, 0.0, 15, -1))
    gps("pi", 8, [], ["pi"], lambda: g.iota(T.pi[:, 0:8], [[0, 8]], 0, 1))
    gps("rows", 16, [], ["rows"], lambda: g.iota(T.oh[:, 0:16], [[1, 16]], 0, 0, allow_small_or_imprecise_dtypes=True))
    act("nJ", 128, ["J"], ["nJ"], scaled(M("nJ"), M("J"), -1.0))
    act("nJ1", 128, ["J"], ["nJ1"], scaled(M("nJ1"), M("J"), -1.0))
    gps("nJ2", 128, ["nJ1"], ["nJ1"], put(M("nJ1"), dia, -2.0, 0))
    gps("nJ3", 128, ["nJ1"], ["nJ1"], put(M("nJ1"), [[-16, 8], [-1000, 16]], -3.0, 0))
    for nm, src, k in (("B", "Bk", 2048.0), ("IP", "I", PEN), ("I2", "I", 256.0), ("MG", "I", MAGIC),
                       ("nMG", "I", -MAGIC), ("nI", "I", -1.0), ("nQ", "I", -16384.0), ("JB", "J", BIG), ("nJB", "J", -BIG),
                       ("K1", "Bk", BIG), ("nK1", "Bk", -BIG), ("IB", "I", BIG), ("nIB", "I", -BIG)):
        act(nm, 128, [src], [nm], scaled(M(nm), M(src), k))
    vec("pj", 8, ["pi"], ["pj"], ts(T.pi[:, 8:16], T.pi[:, 0:8], 15, ALU.bitwise_and))
    vec("pu", 8, ["pj"], ["pu"], lambda: V.tensor_copy(T.pu[:, 0:8], T.pi[:, 8:16]))
    vec("pf", 1, ["pj"], ["pf"], lambda: V.tensor_copy(col(0), T.pi[:, 8:9]))
    vec("oh", 16, ["pf", "rows"], ["oh"], ts(T.oh[:, 16:32], T.oh[:, 0:16], col(0), ALU.is_equal))
    vec("thr", 1, ["oh"], ["thr"], ts(col(1), oh(0), 192.0, ALU.mult))
    vec("win", 1, ["oh"], ["win"], ts(col(3), oh(0), 0.0, ALU.mult))
    vec("stf", 1, ["sti"], ["stf"], ts(col(2), T.sti[:, 0:1], 64.5, ALU.add))
    vec("cSame", 1, ["oh"], ["cSame"], ts(col(4), oh(0), oh(1), ALU.add, oh(15), ALU.subtract))
    vec("cDiff", 1, ["oh"], ["cDiff"], ts(col(5), oh(0), oh(1), ALU.subtract))
    vec("cK0", 1, ["oh"], ["cK0"], ts(col(6), oh(15), oh(0), ALU.subtract))
    vec("cE", 1, ["oh"], ["cE"], ts(col(7), oh(0), 4096.0, ALU.mult))
    vec("cnE", 1, ["oh"], ["cnE"], ts(col(8), oh(0), 4096.0, ALU.mult, -4096.0, ALU.add))
    act("nE", 128, ["I", "cnE"], ["nE"], scaled(M("nE"), M("I"), col(8)))
    act("IK", 128, ["I", "oh"], ["IK"], scaled(M("IK"), M("I"), oh(0)))
    for nm, k in (("Same", 4), ("Diff", 5), ("K0", 6)):
        act(nm, 128, ["JB", "c" + nm], [nm], scaled(M(nm), M("JB"), col(k)))
        act("n" + nm, 128, ["nJB", "c" + nm], ["n" + nm], scaled(M("n" + nm), M("nJB"), col(k)))
    vec("Th0", 64, [], ["Th"], fill(M("Th"), 0.0))
    vec("Th1", 8, ["Th", "J", "oh"], ["Th1"], ts(Mc("Th", 0, 128, 16), Mc("J", 0, 128, 16), oh(15), ALU.mult, 192.0, ALU.mult))
    vec("Th2", 8, ["Th", "J", "cK0"], ["Th2"], ts(Mc("Th", 1, 128, 16), Mc("J", 1, 128, 16), col(6), ALU.mult, 512.0, ALU.mult))
    vec("D0", 16, ["IP"], ["DA"], tt(D(0, 128, 136), Mc("IP", 0, 128, 16), Mc("IP", 15, 128, 16), ALU.subtract))
    vec("D6", 254, ["IP"], ["DB"], tt(D(0, 1, 128), Mc("IP", 1, 128), Mc("IP", 0, 127), ALU.subtract))
    vec("D7", 8, ["DB"], ["DB"], fill(D(0, 0, 128, 16), 0.0))
    for k, nm in enumerate("UV"):
        b = "ps%d" % (3 + k)
        add("V", nm + "1", ("gat", 128), ["pu", nm.lower(), "J"], [nm + "1"],
            tt(M(nm + "1"), T.uv[:, 16 * k:16 * k + 16].indirect(T.pu[:, 0:8]), M("J"), ALU.mult))
        vec(nm + "T", 64, [nm + "1"], [nm + "T"], lambda nm=nm: V.transpose(M(nm + "T"), M(nm + "1")))
        pe(nm + "dp", [(T[b][:, 0:DW], M(nm + "T"), D(0))], [nm + "T", "DA", "DB"], b, True, True, DW)
        act(nm + "d", DW, [], [nm + "d"], scaled(D(1 + k), T[b][:, 0:DW], -16.0 / PEN), [b])
    act("C0", 128, ["J"], ["C"], scaled(D(3, 0, 128), M("J"), -4096.0))
    act("C1", 8, ["J", "C"], ["C1"], scaled(D(3, 0, 128, 16), Mc("J", 0, 128, 16), 2.0 ** 42))
    act("C2", 8, ["J"], ["C2"], scaled(D(3, 128, DW), Mc("J", 0, 128, 16), 15 * 4096.0))
    pe("Cp", [(T.ps5[:, 0:DW], M("nE"), D(0)), (T.ps5[:, 0:DW], M("IK"), D(3))], ["nE", "IK", "DA", "DB", "C1", "C2"], "ps5", True, True, DW)
    act("C", DW, ["C1", "C2"], ["C"], scaled(D(3), T.ps5[:, 0:DW], -1.0 / 4096), ["ps5"])
    vec("zer", 68, [], ["zer"], fill(D(4, 0, 136), 0.0))
    for k in range(2):
        vec("rb%d" % k, 128, [], ["rb%d" % k], fill(T.rb[:, 128 * k:128 * k + 128], 0.0))
    vec("flo0", 8 * n, [], cols("flo0", 0, 16 * n), fill(T.flo[:, 0:16 * n], 0.0))
    for k in range(1, ND1):
        add("S", "flo%d" % k, ("d", 2.5), cols("flo0", 0, 16 * n), cols("flo%d" % k, 0, 16 * n),
            lambda k=k: g.sync.dma_start(T.flo[:, 16 * n * k:16 * n * (k + 1)], T.flo[:, 0:16 * n]), token=("flo", 16 * (ND1 - 1)))

    def land(t, c, what):
        o = (t * LN + c * n) * 3
        k = {"S": 0 if t % 2 == 0 else 2, "E": 1, "b": 2 if t % 2 == 0 else 0}[what]
        return T.land[:, o + k * n:o + (k + 1) * n]

    vec("sqi", LN, ["posi"], ["sqi"], ts(T.sqi[:], T.posi[:], 127, ALU.bitwise_and))
    vec("kni", LN, ["posi"], ["kni"], ts(T.kni[:], T.posi[:], 1920, ALU.bitwise_and))
    vec("K0", LN, ["kni"], ["kin0"], ts(T.kin[:, 0:LN], T.kni[:], -128.0, ALU.add))
    vec("L0", LN, ["posi"], ["L0_%d" % c for c in range(NCH)], lambda: V.tensor_copy(T.lst[:, 0:LN], T.posi[:]))
    for c in range(NCH):
        vec("S0_%d" % c, n, ["sqi"], ["S0_%d" % c], ts(land(0, c, "S"), T.sqi[:, c * n:c * n + n], 128.0, ALU.add))
        vec("E0_%d" % c, n, ["posi", "cE"], ["E0_%d" % c], ts(land(0, c, "E"), T.posi[:, c * n:c * n + n], col(7), ALU.is_le))
        for t in range(PLIES):
            act("b%d_%d_0" % (t, c), n, ["one", "oh"], ["b%d_%d" % (t, c)], scaled(land(t, c, "b"), Mc("one", 0, n), oh(0)))

    def dst(k):
        rid, pid = topo.addr(T.cores[(rank + k) % N], core)
        return DstId(rid=rid, pnc=pid)

    wide = topo.mask(core, T.cores[(rank + 1) % N])
    for k in range(2, PLIES):
        wide &= topo.mask(core, T.cores[(rank + k) % N])
    ne = bin(wide).count("1")

    def ksend():
        tr = RemoteDMATransfer(dst_ids=[dst(k) for k in range(1, PLIES)], dma_engine_mask=wide, remote_sem=T.sem.karr,
                               src=T.kin[:, 0:LN], dsts=[T.kin[:, k * LN:(k + 1) * LN] for k in range(1, PLIES)])
        return g.remote_dma_fused([tr], local_sem=T.sem.kgo)
    ks = add("G", "ksend", ("r", 1), ["kin0"], [], ksend, token=("kgo", ne))
    add("X", "karr", ("x", 2), [], ["kin%d" % k for k in range(1, PLIES)], None, token=("karr", ne * (PLIES - 1)), after=ks)

    step = [0]

    def ply(t, c):
        last = t == PLIES - 1
        q, p = "%d_%d" % (t, c), "%d_%d" % (t - 1, c)
        c0 = c * n
        cs = slice(c0, c0 + n)
        turn = (t * NCH + c) % 2

        def pl(buf, s):
            return buf[:, s * LN + c0:s * LN + c0 + n]

        def L(s):
            return pl(T.lst, s)

        def H(s):
            return pl(T.hh, s)
        Sp, Ep, bp, Kp = land(t, c, "S"), land(t, c, "E"), land(t, c, "b"), pl(T.kin, t)
        rS, rE, rK = "S" + q, "E" + q, "kin%d" % t

        def X(s, i=0, j=n):
            return T.xs[:, 16 * (s * LN + c0 + i) + 15:16 * (s * LN + c0 + j):16]

        def rx(s, i=0, j=n):
            return cols("x%d_%d" % (s, c), 16 * i, 16 * j)

        def wipe(out, nm, s):
            return [(out, M(nm), H(s)), (out, M("n" + nm), H(s))]

        def other(out, Z, kind):
            terms = []
            for s in range(1, t):
                if s in PAR["keep"][kind]:
                    terms = [(out, M("I"), kept(kind, s))] + wipe(out, "Diff", s) + [(out, M("I"), Z(s - 1))]
                elif s == 1:
                    terms = [(out, M("I"), Z(0))] + wipe(out, "Same", 1)
                else:
                    terms += [(out, M("nI"), Z(s - 1))] + wipe(out, "Diff", s) + [(out, M("I"), Z(s - 1))]
            return terms + [(out, M("nI"), Z(t - 1))]

        def kept(kind, s):
            return pl(T.zs, s + PLIES * (kind == "a"))
        o0 = 2 * c0
        ones = Mc("one", 0, n)
        thr, raw, old, a0 = T.ps5[:, 0:n], T.ps0[:, 0:n], T.ps1[:, 0:n], T.ps2[:, 0:n]
        rem, ins = T.ps4[:, 0:n], T.ps4[:, n:2 * n]
        if t == 0:
            vec("H" + q, n // 2, [rS, "thr"], ["H" + q], ts(H(0), Sp, col(1), ALU.is_ge))
            pe("offp" + q, [(old, M("I"), L(0)), (old, M("B"), H(0))], ["I", "B", "L" + q, "H" + q], "ps1", True)
            vec("off" + q, n, [], ["off%d" % c], lambda: V.tensor_copy(T.off[:, o0 + n:o0 + 2 * n], old), ["ps1"])
        else:
            rh = ["I", "nI", "Same", "nSame", "Diff", "nDiff"] + ["H%d_%d" % (s, c) for s in range(t)]
            rl = ["L%d_%d" % (s, c) for s in range(t)]

            def ahead(kind, out, Z, reads, bank):
                keep = t in PAR["keep"][kind]
                pe("pre" + kind + q, other(out, Z, kind), rh + reads + ["Z%s%d_%d" % (kind, s, c) for s in range(t)], bank, True, keep)
                if keep:
                    z = "Z" + kind + q
                    vec(z, n, [], [z], lambda: V.tensor_copy(kept(kind, t), out), [bank])
                    pe("re" + kind + q, [(out, M("I"), kept(kind, t))], [z], bank, True, False)
            pe("thr" + q, [(thr, M("Th"), H(t - 1))], ["Th1", "Th2", "H" + p], "ps5", True)
            vec("H" + q, n, [rS], ["H" + q], tt(H(t), Sp, thr, ALU.is_ge), ["ps5"])
            pe("Re" + q, [(raw, M("I"), Kp)], [rK, "I"], "ps0", True, False)
            pe("R" + q, [(raw, M("I"), Sp), (raw, M("nE"), Ep)], [rS, rE, "nE"], "ps0")
            vec("L" + q, n, [], ["L" + q], ts(L(t), raw, 0.0, ALU.max), ["ps0"])
            ahead("c", old, L, rl, "ps1")
            pe("Op" + q, wipe(old, "Same", t) + [(old, M("I"), L(t - 1))], ["H" + q], "ps1")
            eq = T.eq[:, cs]
            vec("eq" + q, n, ["L" + q], ["eq%d" % c], tt(eq, L(t), old, ALU.is_equal), ["ps1"])
            pe("prer" + q, [(rem, M("I"), kept("c", t))] if t in PAR["keep"]["c"] else other(rem, L, "c"),
               rh + rl + ["Zc%d_%d" % (s, c) for s in range(t + 1)], "ps4", True, False)
            pe("offe" + q, wipe(rem, "Same", t) + [(rem, M("I"), L(t - 1)), (rem, M("B"), H(t)), (ins, M("B"), H(t))],
               ["B", "H" + q], "ps4", False, False)
            pe("offp" + q, [(ins, M("I"), L(t)), (rem, M("nQ"), eq), (ins, M("nQ"), eq)], ["nQ", "eq%d" % c, "L" + q], "ps4")
            vec("off" + q, 2 * n, [], ["off%d" % c], lambda: V.tensor_copy(T.off[:, o0:o0 + 2 * n], T.ps4[:, 0:2 * n]), ["ps4"])
            ahead("a", a0, X, sum([rx(s) for s in range(t)], []), "ps2")
            pe("posa" + q, wipe(a0, "Same", t) + [(a0, M("I"), X(t - 1))], ["H" + q], "ps2", False, False)

        def closing(kind, Z, reads, outbuf, dram):
            early, late = [], []
            for b in range(2):
                out = T.ps7[:, b:2 * n:2]
                early += [(out, M("I"), kept(kind, t))] + wipe(out, "K%d" % b, t - 1) + [(out, M("I"), Z(t - 1))]
                late += [(out, M("nI"), Z(t))] + wipe(out, "K%d" % b, t) + [(out, M("I"), Z(t))]
            pe("Ce" + kind + q, early, ["Z" + kind + q, "K0", "nK0", "K1", "nK1"], "ps7", True, False)
            pe("Cl" + kind + q, late, reads + ["H" + q], "ps7")
            act("o" + kind + q, 2 * n, [], ["o" + kind + q], scaled(outbuf[:, o0:o0 + 2 * n], T.ps7[:, 0:2 * n], 1.0), ["ps7"])
            add("S", "st" + kind + q, ("d", 2.0), ["o" + kind + q], [],
                lambda: g.sync.dma_start(dram[:, o0:o0 + 2 * n], outbuf[:, o0:o0 + 2 * n]), token=("outs", 16 * 3 * NCH))

        if last:
            closing("c", L, ["L" + q], T.oc, T.yc)

        for half in range(int(t == 0), 2):
            d = step[0] % ND1
            step[0] += 1
            f0, g0, s = 16 * n * d, 16 * (2 * c0 + half * n), t if half else PLIES
            i = 0
            for h, part in enumerate(pieces(n, *PAR.get("gat%s_%d" % (q, half), PAR["gat0" if t == 0 else "gat%d" % (1 + half)]))):
                i0 = i
                for e, k in part:
                    j = i + k
                    src = T.tab[:].indirect(T.off[:, o0 + half * n + i:o0 + half * n + j])
                    out = T.gw[:, g0 + 16 * i:g0 + 16 * j]
                    sign = 2.0 * half - 1.0
                    add(e, "gat%s_%d_%d" % (q, half, i), ("gat", 16 * k), ["tab0", "tab1", "none0", "none1", "off%d" % c], cols("gw%d_%d" % (c, half), 16 * i, 16 * j),
                        scaled(out, src, sign) if e == "A" else ts(out, src, sign, ALU.mult))
                    i = j
                m, qh = i - i0, "%s_%d_%d" % (q, half, h)
                rg, rf = cols("gw%d_%d" % (c, half), 16 * i0, 16 * i), cols("flo%d" % d, 16 * i0, 16 * i)
                first = T.gw[:, g0 + 16 * i0:g0 + 16 * i:16]
                ffirst = T.flo[:, f0 + 16 * i0:f0 + 16 * i:16]
                if t == 0:
                    vec("d1" + qh, m // 2, rg, rf, ts(ffirst, first, 0.0, ALU.max))
                else:
                    B = "ps7" if half and not last else "ps2"
                    to = T[B][:, i0:i]
                    pe("d1p" + qh, [(to, M("I"), X(PLIES, i0, i))] * half + [(to, M("I"), first)], rg + rx(PLIES, i0, i) * half, B, half == 1)
                    vec("d1" + qh, m, [], rf, ts(ffirst, to, 0.0, ALU.max), [B])
                if PAR["reset"][half] == "G":
                    gps("rst" + qh, m, [], rg, lambda first=first, m=m: g.iota(first, [[0, m]], -1024, 0, allow_small_or_imprecise_dtypes=True))
                else:
                    vec("rst" + qh, m // 2, [], rg, fill(first, -1024.0))
                for a in range(i0, i, PAR["run"][half]):
                    b = min(i, a + PAR["run"][half])
                    vec("scan" + qh, 8 * (b - a), cols("gw%d_%d" % (c, half), 16 * a, 16 * b) + cols("flo%d" % d, 16 * a, 16 * b), rx(s, a, b),
                        lambda xo=T.xs[:, 16 * (s * LN + c0 + a):16 * (s * LN + c0 + b)], w=T.gw[:, g0 + 16 * a:g0 + 16 * b],
                        floor=T.flo[:, f0 + 16 * a:f0 + 16 * b]: V.tensor_tensor_scan(xo, w, floor, 0.0, ALU.add, ALU.max))
        y = T.yv[:, cs]
        vec("y" + q, n // 2, rx(t), ["y%d" % c], ts(y, X(t), 127.0, ALU.min))
        if last:
            closing("a", X, rx(t), T.oa, T.ya)
        Sc, G, A = "ps3", "ps6", "ps6"
        sc, pg, pa, pz = T[Sc], T[G], T[A][:, 128:128 + n], T[A][:, 192:192 + n]
        ro, di = (0, n) if t % 2 == 0 else (n, 0)
        eb = (t * LN + c0) * 3 + n - ro
        pe("sce" + q, [(sc[:, 0:DW], T.land[:, eb:eb + 2 * n], D(3))], ["C", rE, "b" + q], Sc, True, False, DW)
        pe("scp" + q, [(sc[ro:ro + n, 0:DW], y, D(1)), (sc[di:di + n, 0:DW], y, D(2))], ["y%d" % c, "Ud", "Vd"], Sc, False, 2, DW)
        r0 = 128 * turn
        z = T.zz[:, r0:r0 + 128]
        vec("lap1" + q, 128, ["zer"], ["ra%d" % turn],
            lambda: V.tensor_tensor_scan(T.ra[:, r0:r0 + 128], sc[:, 0:128], D(4, 0, 128), 0.0, ALU.add, ALU.max), [Sc])
        vec("round" + q, 8, ["ra%d" % turn], ["rb%d" % turn],
            tt(T.rb[:, r0:r0 + 128:16], T.ra[:, r0 + 15:r0 + 128:16], sc[:, 128:DW], ALU.add), [Sc])
        vec("lap2" + q, 128, ["rb%d" % turn], ["z%d" % turn],
            lambda: V.tensor_tensor_scan(z, sc[:, 0:128], T.rb[:, r0:r0 + 128], 0.0, ALU.add, ALU.max), [Sc])
        pe("Gr" + q, [(pg[:, 0:128], z, M("I2"))], ["z%d" % turn, "I2"], G, True, True, 128)
        vec("b" + q, n, [rS], ["b" + q], tt(bp, pg[:, ro:ro + n], Sp, ALU.min), [G])
        sth = T.sth[:, cs]
        vec("sth" + q, n, ["stf", "win"], ["sth%d" % c], ts(sth, pg[:, di:di + n], col(3), ALU.is_equal, col(2), ALU.mult), [G])
        pe("raw" + q, [(pa, M("nJ"), Sp), (pa, M("J"), bp), (pa, M("nJ"), sth), (pa, M("MG"), ones), (pa, M("nMG"), ones),
                       (pa, M("J"), Sp), (pa, M("nJ1"), bp), (pa, M("J"), sth)],
           ["J", "nJ", "nJ1", "MG", "nMG", "b" + q, "sth%d" % c], A, True)
        ob = 3 * c0
        hit = T.outb[:, ob + n:ob + 2 * n]
        mov = T.outb[:, ob + 2 * n:ob + 3 * n] if t % 2 == 0 else T.outb[:, ob:ob + n]
        vec("hit" + q, n, [], ["hit%d" % c], ts(hit, pa, -191.5, ALU.is_equal), [A])
        vec("mov" + q, n, [], ["mov%d" % c], ts(mov, pa, 191.5, ALU.add), [A])
        if not last:
            u = "%d_%d" % (t + 1, c)
            lo, lo1, h = (t * LN + c0) * 3, ((t + 1) * LN + c0) * 3, n if t % 2 == 0 else 0

            def onward():
                tr = RemoteDMATransfer(dst_ids=[dst(1)], dma_engine_mask=wide, remote_sem=T.sem["arr" + u],
                                       srcs=[T.outb[:, ob + h:ob + h + 2 * n], T.land[:, lo + h:lo + h + 2 * n]],
                                       dst=T.land[:, lo1 + h:lo1 + h + 2 * n], alu_op=2)
                return g.remote_dma_fused([tr], local_sem=T.sem["go%d" % c])
            s = add("G", "snd" + q, ("r", 1), ["mov%d" % c, "hit%d" % c, "b" + q, rE], [], onward, token=("go%d" % c, ne * (t + 1)))
            add("X", "arr" + u, ("x", 1), [], ["S" + u, "E" + u], None, token=("arr" + u, ne), after=s)
        else:
            pe("ylp" + q, [(pz, M("I"), mov), (pz, M("IB"), bp), (pz, M("nIB"), bp), (pz, M("I"), bp), (pz, M("I"), Kp),
                           (pz, M("nE"), Ep), (pz, M("nE"), hit)], ["IB", "nIB", rK, rE, "mov%d" % c, "hit%d" % c], A, True)
            act("yl" + q, n, [], ["ol%d" % c], lambda: S.activation(T.ol[:, cs], pz, ACT.Relu), [A])
            add("S", "stl" + q, ("d", 2.0), ["ol%d" % c], [], lambda: g.sync.dma_start(T.yl[:, cs], T.ol[:, cs]),
                token=("outs", 16 * 3 * NCH))

    now.append(True)
    for t in range(PLIES):
        for c in range(NCH):
            now[0] = (t, c)
            ply(t, c)
    return ops


def depend(ops):
    wr, rd, run = {}, {}, {}
    deps = []
    for i, o in enumerate(ops):
        d = set()
        for x in o["r"]:
            if x in wr:
                d.add(wr[x])
        for x in o["w"]:
            if x in wr:
                d.add(wr[x])
            d.update(rd.get(x, []))
        for b in o["banks"]:
            e, cur, prev = run.get(b, (None, [], []))
            if e == o["eng"]:
                d.update(prev)
                cur.append(i)
            else:
                d.update(cur)
                run[b] = (o["eng"], [i], cur)
        for x in o["r"]:
            rd.setdefault(x, []).append(i)
        for x in o["w"]:
            wr[x] = i
            rd[x] = []
        d.discard(i)
        deps.append(sorted(d))
    return deps


def waits(ops, i, j):
    return not (ops[i]["eng"] == "P" and ops[j]["eng"] == "P")


def times(o, par):
    k, x = o["cost"]
    if k == "v":
        a = par["fix"] + x * par["cyc"]
        return a, a
    if k == "gat":
        a = 0.06 + x * par["gat"] * par["cyc"]
        return a, a
    if k == "g":
        a = 0.16 + 2 * x * par["cyc"]
        return a, a
    if k == "p":
        a = x * par["pe"]
        return a, a + par["pefix"]
    if k == "d":
        return 0.1, x
    if k == "r":
        return par["issue"], par["wire"]
    return 0.0, par["wire"] * x


def schedule(ops, deps, par):
    m = len(ops)
    tm = [times(o, par) for o in ops]
    nxt = [[] for _ in ops]
    for i in range(m):
        for j in deps[i]:
            nxt[j].append(i)
    way = [0.0] * m
    for i in range(m - 1, -1, -1):
        t, c = ops[i]["chunk"]
        due = -(c * par["beat0"] if t == 0 else NCH * par["beat0"] + ((t - 1) * NCH + c) * par["beat"])
        way[i] = max([way[j] + par["hop"] for j in nxt[i]] or [due]) + tm[i][1]
        if ops[i]["name"].startswith("snd"):
            way[i] = due + tm[i][1]
        if ops[i]["name"] == "ksend":
            way[i] = par["kway"]
    done, left = [None] * m, [len(d) for d in deps]
    ready = [0.0] * m
    free = {e: 0.0 for e in "VAPGS"}
    pool = {e: [i for i in range(m) if ops[i]["eng"] == e and not left[i]] for e in "VAPGS"}
    arrive = {o["after"]: i for i, o in enumerate(ops) if o["after"] is not None}
    order = []

    def finish(i, begun, at):
        done[i] = at
        for j in nxt[i]:
            ready[j] = max(ready[j], at + par["hop"] if waits(ops, j, i) else begun)
            left[j] -= 1
            if not left[j]:
                pool[ops[j]["eng"]].append(j)
    while any(pool.values()):
        e = min((x for x in pool if pool[x]), key=lambda x: max(free[x], min(ready[i] for i in pool[x])))
        now = max(free[e], min(ready[i] for i in pool[e]))
        i = max((j for j in pool[e] if ready[j] <= now + par["look"]), key=lambda j: (way[j], -j))
        pool[e].remove(i)
        now = max(now, ready[i])
        free[e] = now + tm[i][0]
        order.append(i)
        finish(i, now, now + tm[i][1])
        if i in arrive:
            order.append(arrive[i])
            finish(arrive[i], now, now + tm[arrive[i]][1])
    return justify(ops, deps, par, order)


def justify(ops, deps, par, order):
    m = len(ops)
    tm = [times(o, par) for o in ops]
    pre = [[(j, tm[j][1] + par["hop"] if waits(ops, i, j) else tm[j][0]) for j in deps[i]] for i in range(m)]
    for i, o in enumerate(ops):
        if o["after"] is not None:
            pre[i] = [(o["after"], 0.0)]
    suc = [[] for _ in ops]
    for i in range(m):
        for j, lag in pre[i]:
            suc[j].append((i, lag))

    def pack(seq, back):
        at, busy = [0.0] * m, {}
        for i in seq:
            hold = tm[i][0]
            s = max([at[j] + lag for j, lag in suc[i]] + [tm[i][1]]) - hold if back else max([at[j] + lag for j, lag in pre[i]] + [0.0])
            if hold:
                line = busy.setdefault(ops[i]["eng"], [])
                k = 0
                for k, (a, b) in enumerate(line + [(1e9, 1e9)]):
                    if s + hold <= a + 1e-9:
                        break
                    s = max(s, b)
                line.insert(k, (s, s + hold))
            at[i] = s + hold if back else s
        return at
    best = None
    for _ in range(par["passes"]):
        at = pack(order, False)
        rank = {i: k for k, i in enumerate(order)}
        order = sorted(order, key=lambda i: (at[i], rank[i]))
        end = max(at[i] + tm[i][1] for i in range(m))
        if best is None or end < best[1]:
            best = (order, end, [at[i] + tm[i][1] for i in range(m)])
        rank = {i: k for k, i in enumerate(order)}
        late = pack(sorted(order, key=lambda i: (-at[i], -rank[i])), True)
        order = sorted(order, key=lambda i: (-late[i], rank[i]))
    return best


def polish(ops, deps, par, order):
    m = len(ops)
    rng = np.random.default_rng(par["seed"])
    eng = ["VAPGSX".index(o["eng"]) for o in ops]
    pre, hold, res = [], [], []
    for _, guess in COSTS:
        cost = dict(par, **guess)
        tm = [times(o, cost) for o in ops]
        pre.append([[(o["after"], 0.0)] if o["after"] is not None else
                    [(j, tm[j][1] + cost["hop"] if waits(ops, i, j) else 0.0) for j in deps[i]] for i, o in enumerate(ops)])
        hold.append([x[0] for x in tm])
        res.append([x[1] for x in tm])
    before = [set(j for j, _ in pre[0][i]) for i in range(m)]
    after = [set() for _ in ops]
    for i in range(m):
        for j in before[i]:
            after[j].add(i)
    ends = [i for i in range(m) if not after[i]]

    def run(seq, k, r, old):
        at, by = (list(old[1]), list(old[2])) if old else ([0.0] * m, [-1] * m)
        free, last = [0.0] * 6, [-1] * 6
        for i in seq[:r]:
            free[eng[i]], last[eng[i]] = at[i] + hold[k][i], i
        for i in seq[r:]:
            e = eng[i]
            s, w = (0.0, -1) if e == 5 else (free[e], -2 - last[e])
            for j, lag in pre[k][i]:
                if at[j] + lag > s:
                    s, w = at[j] + lag, j
            at[i], by[i] = s, w
            free[e], last[e] = s + hold[k][i], i
        return max((at[i] + res[k][i], i) for i in ends), at, by

    def pairs(x):
        out, i = [], x[0][1]
        while i >= 0:
            w = x[2][i]
            if w <= -2:
                out.append((-2 - w, i))
            i = -2 - w if w <= -2 else w
        return out

    def score(seq, r, old):
        rs = [run(seq, k, r, old and old[k]) for k in range(len(COSTS))]
        return sum(c[0] * x[0][0] for c, x in zip(COSTS, rs)), rs
    cur, rs = score(order, 0, None)
    best, crit = (cur, order), [pairs(x) for x in rs]
    for u in rng.random((par["tries"], 5)).tolist():
        a = crit[int(u[0] * len(COSTS))]
        if not a:
            continue
        j, i = a[int(u[1] * len(a))]
        r, p = order.index(j), order.index(i)
        far, up = max(0, int(u[2] * 3)), u[3] < 0.5
        while far and (r > 0 if up else p < m - 1):
            r, p = (r - 1, p) if up else (r, p + 1)
            far -= eng[order[r if up else p]] == eng[i]
        mid = order[r:p + 1]
        along = {i if up else j}
        for x in (reversed(mid) if up else mid):
            if (after if up else before)[x] & along:
                along.add(x)
        if (j if up else i) in along:
            continue
        new = order[:r] + [x for x in mid if (x in along) == up] + [x for x in mid if (x in along) != up] + order[p + 1:]
        c, nr = score(new, r, rs)
        if c <= cur or u[4] < math.exp((cur - c) / par["warm"]):
            order, cur, rs = new, c, nr
            crit = [pairs(x) for x in rs]
            if c < best[0]:
                best = (c, order)
    return best[1]


PLAN = {}


def rank_program(g, core, T, topo):
    if T.rank_of(core) is None:
        return
    ops = build(g, T, core, topo)
    if not PLAN:
        PLAN["deps"] = depend(ops)
        PLAN["order"] = polish(ops, PLAN["deps"], PAR, schedule(ops, PLAN["deps"], PAR)[0])
    deps = PLAN["deps"]
    queue = {"V": g.vector, "A": g.scalar, "P": g.tensor, "G": g, "S": g.sync}
    known = {e: {} for e in queue}
    count = {e: 0 for e in queue}
    token, clock, total = {}, {}, {}
    for i in PLAN["order"]:
        o = ops[i]
        e = o["eng"]
        if e == "X":
            token[i] = o["token"]
            clock[i] = {o["token"][0]: o["token"][1]}
            total[o["token"][0]] = o["token"][1]
            continue
        kn = known[e]
        for j in sorted(deps[i], key=lambda j: -token[j][1]):
            s, v = token[j]
            if kn.get(s, 0) < v and waits(ops, i, j):
                queue[e].wait_ge(T.sem[s], v)
                for a, b in clock[j].items():
                    kn[a] = max(kn.get(a, 0), b)
        ins = o["fn"]()
        if o["token"] is None:
            count[e] += 1
            token[i] = ("c" + e, count[e])
            ins.then_inc(T.sem["c" + e], 1)
        else:
            token[i] = o["token"]
            if o["cost"][0] == "d":
                ins.then_inc(T.sem[o["token"][0]], 16)
        clock[i] = dict(kn)
        clock[i][token[i][0]] = token[i][1]
        total[token[i][0]] = max(total.get(token[i][0], 0), token[i][1])
    seen = {}
    for kn in known.values():
        for a, b in kn.items():
            seen[a] = max(seen.get(a, 0), b)
    for s, v in total.items():
        if seen.get(s, 0) < v:
            g.sync.wait_ge(T.sem[s], v)
